import numpy as np
import ml_dtypes


def mxq(x, axis, fmt="e4m3"):
    dtype, down = {"e4m3": (ml_dtypes.float8_e4m3fn, 7), "e5m2": (ml_dtypes.float8_e5m2, 14)}[fmt]
    v = np.moveaxis(np.asarray(x, np.float32).astype(ml_dtypes.bfloat16).astype(np.float64), axis, -1)
    blocks = v.reshape(v.shape[:-1] + (-1, 32))
    amax = np.abs(blocks).max(-1, keepdims=True)
    byte = np.maximum(np.where(amax > 0, np.frexp(amax)[1] - 1 + 127, 0) - down, 1)
    scale = np.exp2(byte - 127.0)
    codes = (blocks / scale).astype(np.float32).astype(dtype).astype(np.float64)
    return np.moveaxis((codes * scale).reshape(v.shape), -1, axis)


WIDE = False


def mx_kscale(k):
    if not WIDE:
        return np.ones(k)
    levels = np.array([10, -10, 5, -5, 0])
    if k % 512:
        return np.exp2(np.random.permutation(np.resize(levels, k // 32))).repeat(32)
    a = np.empty((k // 512, 16))
    for p in range(k // 512):
        a[p, :8] = np.random.permutation(np.resize(levels, 8))
        for g in range(8):
            far = levels[np.abs(levels - a[p, g]) >= 10]
            a[p, g + 8] = far[np.random.randint(len(far))]
    return np.exp2(a.ravel()).repeat(32)


def f64(x):
    return np.asarray(x).astype(np.float64)


def striped(idx):
    return np.tile(idx.reshape(-1, 16).T, (8, 1)).astype(np.uint16)


def unstriped(offs):
    return offs[:16].T.reshape(-1).astype(np.int64)


def pack_weight(w):
    k, n = w.shape
    w = f64(np.asarray(w, np.float32).astype(ml_dtypes.bfloat16)).reshape(k // 32, 32, n)
    amax = np.abs(w).max(1)
    byte = np.clip(np.where(amax > 0, np.frexp(amax)[1] - 1 + 127 - 7, 1), 1, 254)
    scaled = (w * np.exp2(127.0 - byte)[:, None, :]).reshape(k, n).astype(np.float32)
    words = np.ascontiguousarray(scaled.reshape(k // 512, 128, 4, n).transpose(0, 1, 3, 2)).astype(ml_dtypes.float8_e4m3fn).view(np.uint8)
    return words, np.ascontiguousarray(byte.astype(np.uint8).reshape(k // 512, 16, n))


def unpack_weight(words, scales):
    g, p, n, _ = words.shape
    vals = np.ascontiguousarray(words).view(ml_dtypes.float8_e4m3fn).astype(np.float64) * np.repeat(np.exp2(scales.astype(np.float64) - 127.0), 8, axis=1)[..., None]
    return vals.transpose(0, 1, 3, 2).reshape(g * 512, n)


K, T, E, C, N = 1024, 512, 4, 256, 128


def by_expert(wq, xq):
    return np.concatenate([wq[e].T @ xq[:, e * C:(e + 1) * C] for e in range(E)], axis=1)


def setup_inputs():
    n = np.random.standard_normal
    s = mx_kscale(K)[:, None]
    first = np.random.permutation(np.repeat(np.arange(E), T // E))
    second = (first + 1 + np.random.permutation(np.repeat(np.arange(E - 1), -(-T // (E - 1)))[:T])) % E
    while np.bincount(second, minlength=E).max() != T // E:
        load = np.bincount(second, minlength=E); hi, lo = int(load.argmax()), int(load.argmin())
        t = np.flatnonzero((second == hi) & (first != lo))[0]; second[t] = lo
    slot_token = np.empty(E * C, np.int64); pos = np.empty((2, T), np.int64); fill = np.zeros(E, np.int64)
    place = np.stack([np.random.permutation(C) for _ in range(E)])
    for r, deal in enumerate((first, second)):
        for t in np.random.permutation(T):
            e = deal[t]; j = e * C + place[e, fill[e]]; fill[e] += 1; slot_token[j] = t; pos[r, t] = j
    g = np.random.uniform(0.2, 0.8, T)
    packed = [pack_weight(m) for m in n((E, K, N)) / np.sqrt(K) / s[None]]
    return {
        "xT": (n((K, T)) * s).astype(np.float32),
        "w_words": np.stack([m[0] for m in packed]),
        "w_scales": np.stack([m[1] for m in packed]),
        "b": (0.3 * n((N, E))).astype(np.float32),
        "gate": np.stack([np.tile(g, (N, 1)), np.tile(1.0 - g, (N, 1))]).astype(np.float32),
        "offs": striped(slot_token),
        "pos1": striped(pos[0]),
        "pos2": striped(pos[1]),
    }


def reference(xT, w_words, w_scales, b, gate, offs, pos1, pos2):
    idx = unstriped(offs)
    xq = mxq(f64(xT)[:, idx], 0, "e4m3")
    w = np.stack([unpack_weight(w_words[e], w_scales[e]) for e in range(E)])
    y = by_expert(w, xq)
    y = y + np.repeat(f64(b), C, axis=1)
    return f64(gate[0]) * y[:, unstriped(pos1)] + f64(gate[1]) * y[:, unstriped(pos2)]

@@ -1,0 +1,106 @@
+from contextlib import ExitStack
+
+import concourse.mybir as mybir
+
+K, T, E, C, N = 1024, 512, 4, 256, 128
+FLOPS = 2 * K * N * E * C
+
+F32 = mybir.dt.float32
+BF16 = mybir.dt.bfloat16
+U8 = mybir.dt.uint8
+U16 = mybir.dt.uint16
+U32 = mybir.dt.uint32
+I32 = mybir.dt.int32
+FP8X4 = mybir.dt.float8_e4m3fn_x4
+
+P = 128
+PACK = 4
+PASSES = K // (P * PACK)
+OFFS_COLS = C // 16
+
+
+def tile_routed_moe_kernel(tc, xT, w_words, w_scales, b, gate, offs, pos1, pos2, out):
+    nc = tc.nc
+    mult, add = mybir.AluOpType.mult, mybir.AluOpType.add
+    with ExitStack() as ctx:
+        held = ctx.enter_context(tc.tile_pool(name="held", bufs=1))
+        ring = ctx.enter_context(tc.tile_pool(name="ring", bufs=3))
+        psum = ctx.enter_context(tc.psum_pool(name="psum", bufs=1))
+
+        offs_sb = held.tile([P, E * C // 16], U16, name="offs_sb")
+        nc.sync.dma_start(offs_sb[:], offs)
+
+        x_planes = xT.rearrange("(g p t) n -> g p t n", p=P, t=PACK)
+        planes = {}
+        for g in range(PASSES):
+            for t in range(PACK):
+                planes[(g, t)] = held.tile([P, T], F32, name="plane%d%d" % (g, t))
+                nc.sync.dma_start(planes[(g, t)][:], x_planes[g, :, t, :])
+
+        w_scale_sb = held.tile([P, E * PASSES, N], U8, name="w_scale_sb", align_bytes=64)
+        nc.vector.memset(w_scale_sb[:].rearrange("p j n -> p (j n)").bitcast(I32), 0)
+        scale_rows = w_scales.rearrange("e a (q r) n -> q r (e a) n", r=4)
+        for q in range(4):
+            nc.sync.dma_start(w_scale_sb[32 * q : 32 * q + 4, :, :].bitcast(I32), scale_rows[q].bitcast(I32))
+
+        w_code_sb = held.tile([P, E * PASSES, N * PACK], U8, name="w_code_sb", align_bytes=64)
+        nc.sync.dma_start(w_code_sb[:], w_words.rearrange("e a p n r -> p (e a) (n r)"))
+
+        b_sb = held.tile([P, E], F32, name="b_sb")
+        nc.sync.dma_start(b_sb[:], b)
+        pos1_sb = held.tile([P, T // 16], U16, name="pos1_sb")
+        nc.sync.dma_start(pos1_sb[:], pos1)
+        pos2_sb = held.tile([P, T // 16], U16, name="pos2_sb")
+        nc.sync.dma_start(pos2_sb[:], pos2)
+        gate1_sb = held.tile([P, T], F32, name="gate1_sb")
+        nc.sync.dma_start(gate1_sb[:], gate[0])
+        gate2_sb = held.tile([P, T], F32, name="gate2_sb")
+        nc.sync.dma_start(gate2_sb[:], gate[1])
+
+        x_codes = held.tile([P, PASSES, E * C], U32, name="x_codes", align_bytes=64)
+        x_scales = held.tile([P, PASSES, E * C], U8, name="x_scales", align_bytes=64)
+        y = held.tile([P, E * C], F32, name="y")
+        acc = [psum.tile([P, 512], F32, name="acc%d" % e) for e in range(E)]
+
+        grouped = {}
+
+        def gather(g, e):
+            g4 = ring.tile([P, PACK, C], F32, name="g4")
+            for t in range(PACK):
+                nc.vector.tensor_copy(g4[:, t, :], planes[(g, t)][:].indirect(offs_sb[:, e * OFFS_COLS : (e + 1) * OFFS_COLS]))
+            grouped[(g, e)] = ring.tile([P, C, PACK], BF16, name="grouped", align_bytes=64)
+            nc.scalar.copy(out=grouped[(g, e)][:], in_=g4[:].rearrange("p t n -> p n t"))
+
+        def multiply(g, e):
+            cols = slice(e * C, (e + 1) * C)
+            nc.vector.quantize_mx(
+                out=x_codes[:, g, cols].bitcast(FP8X4),
+                scales=x_scales[:, g, cols],
+                in_=grouped[(g, e)][:].rearrange("p n t -> p (n t)"),
+            )
+            nc.tensor.matmul_mx(
+                out=acc[e][:, 0:C],
+                lhsT=w_code_sb[:, e * PASSES + g, :].bitcast(FP8X4),
+                lhsT_scale=w_scale_sb[:, e * PASSES + g, :],
+                rhs=x_codes[:, g, cols].bitcast(FP8X4),
+                rhs_scale=x_scales[:, g, cols],
+                start=(g == 0),
+                stop=(g == PASSES - 1),
+            )
+            if g == PASSES - 1:
+                nc.scalar.activation(out=y[:, cols], in_=acc[e][:, 0:C], func=mybir.ActivationFunctionType.Identity, bias=b_sb[:, e : e + 1])
+
+        units = [(g, e) for g in range(PASSES) for e in range(E)]
+        for i, (g, e) in enumerate(units):
+            gather(g, e)
+            if i >= 1:
+                multiply(*units[i - 1])
+        multiply(*units[-1])
+
+        part1 = held.tile([P, T], F32, name="part1")
+        part2 = held.tile([P, T], F32, name="part2")
+        result = held.tile([P, T], F32, name="result")
+        nc.vector.tensor_tensor(out=part1[:], in0=y[:].indirect(pos1_sb[:]), in1=gate1_sb[:], op=mult)
+        nc.vector.tensor_tensor(out=part2[:], in0=y[:].indirect(pos2_sb[:]), in1=gate2_sb[:], op=mult)
+        nc.vector.tensor_tensor(out=result[:], in0=part1[:], in1=part2[:], op=add)
+        nc.sync.dma_start(out, result[:])

@@ -22,29 +22,27 @@ OFFS_COLS = C // 16
 def tile_routed_moe_kernel(tc, xT, w_words, w_scales, b, gate, offs, pos1, pos2, out):
     nc = tc.nc
     mult, add = mybir.AluOpType.mult, mybir.AluOpType.add
+    act = mybir.ActivationFunctionType
     with ExitStack() as ctx:
         held = ctx.enter_context(tc.tile_pool(name="held", bufs=1))
-        ring = ctx.enter_context(tc.tile_pool(name="ring", bufs=3))
         psum = ctx.enter_context(tc.psum_pool(name="psum", bufs=1))
 
         offs_sb = held.tile([P, E * C // 16], U16, name="offs_sb")
         nc.sync.dma_start(offs_sb[:], offs)
 
         x_planes = xT.rearrange("(g p t) n -> g p t n", p=P, t=PACK)
-        planes = {}
-        for g in range(PASSES):
-            for t in range(PACK):
-                planes[(g, t)] = held.tile([P, T], F32, name="plane%d%d" % (g, t))
-                nc.sync.dma_start(planes[(g, t)][:], x_planes[g, :, t, :])
+        raw = [held.tile([P, PACK, T], F32, name="raw%d" % g) for g in range(PASSES)]
+        for g, t in ((0, 0), (1, 0), (1, 1), (0, 1), (1, 2), (1, 3), (0, 2), (0, 3)):
+            nc.sync.dma_start(raw[g][:, t, :], x_planes[g, :, t, :])
+
+        w_code_sb = held.tile([P, E * PASSES, N * PACK], U8, name="w_code_sb", align_bytes=64)
+        nc.sync.dma_start(w_code_sb[:], w_words.rearrange("e a p n r -> p (e a) (n r)"))
 
         w_scale_sb = held.tile([P, E * PASSES, N], U8, name="w_scale_sb", align_bytes=64)
         nc.vector.memset(w_scale_sb[:].rearrange("p j n -> p (j n)").bitcast(I32), 0)
         scale_rows = w_scales.rearrange("e a (q r) n -> q r (e a) n", r=4)
         for q in range(4):
             nc.sync.dma_start(w_scale_sb[32 * q : 32 * q + 4, :, :].bitcast(I32), scale_rows[q].bitcast(I32))
-
-        w_code_sb = held.tile([P, E * PASSES, N * PACK], U8, name="w_code_sb", align_bytes=64)
-        nc.sync.dma_start(w_code_sb[:], w_words.rearrange("e a p n r -> p (e a) (n r)"))
 
         b_sb = held.tile([P, E], F32, name="b_sb")
         nc.sync.dma_start(b_sb[:], b)
@@ -61,15 +59,20 @@ def tile_routed_moe_kernel(tc, xT, w_words, w_scales, b, gate, offs, pos1, pos2,
         x_scales = held.tile([P, PASSES, E * C], U8, name="x_scales", align_bytes=64)
         y = held.tile([P, E * C], F32, name="y")
         acc = [psum.tile([P, 512], F32, name="acc%d" % e) for e in range(E)]
-
+        rounded = held.tile([P, PACK, T], BF16, name="rounded")
         grouped = {}
+        for g in range(PASSES):
+            for e in range(E):
+                grouped[(g, e)] = held.tile([P, C, PACK], BF16, name="grouped%d%d" % (g, e), align_bytes=64)
 
-        def gather(g, e):
-            g4 = ring.tile([P, PACK, C], F32, name="g4")
-            for t in range(PACK):
-                nc.vector.tensor_copy(g4[:, t, :], planes[(g, t)][:].indirect(offs_sb[:, e * OFFS_COLS : (e + 1) * OFFS_COLS]))
-            grouped[(g, e)] = ring.tile([P, C, PACK], BF16, name="grouped", align_bytes=64)
-            nc.scalar.copy(out=grouped[(g, e)][:], in_=g4[:].rearrange("p t n -> p n t"))
+        def slots(e):
+            return offs_sb[:, e * OFFS_COLS : (e + 1) * OFFS_COLS]
+
+        def gather_vector(g, t, e):
+            nc.vector.tensor_copy(grouped[(g, e)][:, :, t], raw[g][:, t, :].indirect(slots(e)))
+
+        def gather_scalar(t, e):
+            nc.scalar.activation(grouped[(1, e)][:, :, t], rounded[:, t, :].indirect(slots(e)), act.Copy)
 
         def multiply(g, e):
             cols = slice(e * C, (e + 1) * C)
@@ -88,14 +91,21 @@ def tile_routed_moe_kernel(tc, xT, w_words, w_scales, b, gate, offs, pos1, pos2,
                 stop=(g == PASSES - 1),
             )
             if g == PASSES - 1:
-                nc.scalar.activation(out=y[:, cols], in_=acc[e][:, 0:C], func=mybir.ActivationFunctionType.Identity, bias=b_sb[:, e : e + 1])
+                nc.scalar.activation(out=y[:, cols], in_=acc[e][:, 0:C], func=act.Identity, bias=b_sb[:, e : e + 1])
 
-        units = [(g, e) for g in range(PASSES) for e in range(E)]
-        for i, (g, e) in enumerate(units):
-            gather(g, e)
-            if i >= 1:
-                multiply(*units[i - 1])
-        multiply(*units[-1])
+        for t in range(PACK):
+            nc.scalar.copy(out=rounded[:, t, :], in_=raw[1][:, t, :])
+            for e in range(E):
+                gather_vector(0, t, e)
+            for e in range(E - 1):
+                gather_scalar(t, e)
+        for t in range(PACK):
+            gather_vector(1, t, E - 1)
+            multiply(0, t)
+        multiply(1, 0)
+        multiply(1, E - 1)
+        multiply(1, 1)
+        multiply(1, 2)
 
         part1 = held.tile([P, T], F32, name="part1")
         part2 = held.tile([P, T], F32, name="part2")

@@ -31,9 +31,11 @@ def tile_routed_moe_kernel(tc, xT, w_words, w_scales, b, gate, offs, pos1, pos2,
         nc.sync.dma_start(offs_sb[:], offs)
 
         x_planes = xT.rearrange("(g p t) n -> g p t n", p=P, t=PACK)
-        raw = [held.tile([P, PACK, T], F32, name="raw%d" % g) for g in range(PASSES)]
-        for g, t in ((0, 0), (1, 0), (1, 1), (0, 1), (1, 2), (1, 3), (0, 2), (0, 3)):
-            nc.sync.dma_start(raw[g][:, t, :], x_planes[g, :, t, :])
+        planes = {}
+        for t in range(PACK):
+            for g in (1, 0):
+                planes[(g, t)] = held.tile([P, T], F32, name="plane%d%d" % (g, t))
+                nc.sync.dma_start(planes[(g, t)][:], x_planes[g, :, t, :])
 
         w_code_sb = held.tile([P, E * PASSES, N * PACK], U8, name="w_code_sb", align_bytes=64)
         nc.sync.dma_start(w_code_sb[:], w_words.rearrange("e a p n r -> p (e a) (n r)"))
@@ -60,6 +62,7 @@ def tile_routed_moe_kernel(tc, xT, w_words, w_scales, b, gate, offs, pos1, pos2,
         y = held.tile([P, E * C], F32, name="y")
         acc = [psum.tile([P, 512], F32, name="acc%d" % e) for e in range(E)]
         rounded = held.tile([P, PACK, T], BF16, name="rounded")
+        picked = [held.tile([P, PACK, C], F32, name="picked%d" % e) for e in range(E)]
         grouped = {}
         for g in range(PASSES):
             for e in range(E):
@@ -68,8 +71,11 @@ def tile_routed_moe_kernel(tc, xT, w_words, w_scales, b, gate, offs, pos1, pos2,
         def slots(e):
             return offs_sb[:, e * OFFS_COLS : (e + 1) * OFFS_COLS]
 
-        def gather_vector(g, t, e):
-            nc.vector.tensor_copy(grouped[(g, e)][:, :, t], raw[g][:, t, :].indirect(slots(e)))
+        def gather_vector(t, e):
+            nc.vector.tensor_copy(picked[e][:, t, :], planes[(0, t)][:].indirect(slots(e)))
+
+        def interleave(e):
+            nc.gpsimd.tensor_scalar(out=grouped[(0, e)][:], in0=picked[e][:].rearrange("p t n -> p n t"), scalar1=1.0, scalar2=0.0, op0=mult, op1=add)
 
         def gather_scalar(t, e):
             nc.scalar.activation(grouped[(1, e)][:, :, t], rounded[:, t, :].indirect(slots(e)), act.Copy)
@@ -91,21 +97,34 @@ def tile_routed_moe_kernel(tc, xT, w_words, w_scales, b, gate, offs, pos1, pos2,
                 stop=(g == PASSES - 1),
             )
             if g == PASSES - 1:
-                nc.scalar.activation(out=y[:, cols], in_=acc[e][:, 0:C], func=act.Identity, bias=b_sb[:, e : e + 1])
+                nc.vector.tensor_scalar(out=y[:, cols], in0=acc[e][:, 0:C], scalar1=b_sb[:, e : e + 1], scalar2=None, op0=add)
 
         for t in range(PACK):
-            nc.scalar.copy(out=rounded[:, t, :], in_=raw[1][:, t, :])
-            for e in range(E):
-                gather_vector(0, t, e)
-            for e in range(E - 1):
-                gather_scalar(t, e)
+            nc.gpsimd.tensor_scalar(out=rounded[:, t, :], in0=planes[(1, t)][:], scalar1=1.0, scalar2=0.0, op0=mult, op1=add)
         for t in range(PACK):
-            gather_vector(1, t, E - 1)
-            multiply(0, t)
+            gather_vector(t, 0)
+            gather_vector(t, 1)
+            gather_scalar(t, 0)
+            gather_scalar(t, 1)
+        interleave(0)
+        interleave(1)
+        for t in range(PACK):
+            gather_vector(t, 2)
+        interleave(2)
+        multiply(0, 0)
+        multiply(0, 1)
+        for t in range(PACK):
+            gather_vector(t, 3)
+            gather_scalar(t, 2)
+        interleave(3)
+        multiply(0, 2)
         multiply(1, 0)
-        multiply(1, E - 1)
         multiply(1, 1)
+        for t in range(PACK):
+            gather_scalar(t, 3)
+        multiply(0, 3)
         multiply(1, 2)
+        multiply(1, 3)
 
         part1 = held.tile([P, T], F32, name="part1")
         part2 = held.tile([P, T], F32, name="part2")

@@ -34,7 +34,7 @@ def tile_routed_moe_kernel(tc, xT, w_words, w_scales, b, gate, offs, pos1, pos2,
         planes = {}
         for t in range(PACK):
             for g in (1, 0):
-                planes[(g, t)] = held.tile([P, T], F32, name="plane%d%d" % (g, t))
+                planes[(g, t)] = held.tile([P, T], F32, name="plane%d%d" % (g, t), tag="late" if (g, t) == (1, PACK - 1) else "plane%d%d" % (g, t))
                 nc.sync.dma_start(planes[(g, t)][:], x_planes[g, :, t, :])
 
         w_code_sb = held.tile([P, E * PASSES, N * PACK], U8, name="w_code_sb", align_bytes=64)
@@ -62,31 +62,18 @@ def tile_routed_moe_kernel(tc, xT, w_words, w_scales, b, gate, offs, pos1, pos2,
         y = held.tile([P, E * C], F32, name="y")
         acc = [psum.tile([P, 512], F32, name="acc%d" % e) for e in range(E)]
         rounded = held.tile([P, PACK, T], BF16, name="rounded")
-        picked = [held.tile([P, PACK, C], F32, name="picked%d" % e) for e in range(E)]
-        grouped = {}
-        for g in range(PASSES):
-            for e in range(E):
-                grouped[(g, e)] = held.tile([P, C, PACK], BF16, name="grouped%d%d" % (g, e), align_bytes=64)
+        grouped0 = held.tile([P, E * C, PACK], BF16, name="grouped0", align_bytes=64)
+        grouped1 = [held.tile([P, C, PACK], BF16, name="grouped1%d" % e, align_bytes=64) for e in range(E)]
 
         def slots(e):
             return offs_sb[:, e * OFFS_COLS : (e + 1) * OFFS_COLS]
 
-        def gather_vector(t, e):
-            nc.vector.tensor_copy(picked[e][:, t, :], planes[(0, t)][:].indirect(slots(e)))
-
-        def interleave(e):
-            nc.gpsimd.tensor_scalar(out=grouped[(0, e)][:], in0=picked[e][:].rearrange("p t n -> p n t"), scalar1=1.0, scalar2=0.0, op0=mult, op1=add)
-
-        def gather_scalar(t, e):
-            nc.scalar.activation(grouped[(1, e)][:, :, t], rounded[:, t, :].indirect(slots(e)), act.Copy)
+        def quantize(g, first, count, in_):
+            cols = slice(first * C, (first + count) * C)
+            nc.vector.quantize_mx(out=x_codes[:, g, cols].bitcast(FP8X4), scales=x_scales[:, g, cols], in_=in_)
 
         def multiply(g, e):
             cols = slice(e * C, (e + 1) * C)
-            nc.vector.quantize_mx(
-                out=x_codes[:, g, cols].bitcast(FP8X4),
-                scales=x_scales[:, g, cols],
-                in_=grouped[(g, e)][:].rearrange("p n t -> p (n t)"),
-            )
             nc.tensor.matmul_mx(
                 out=acc[e][:, 0:C],
                 lhsT=w_code_sb[:, e * PASSES + g, :].bitcast(FP8X4),
@@ -96,35 +83,34 @@ def tile_routed_moe_kernel(tc, xT, w_words, w_scales, b, gate, offs, pos1, pos2,
                 start=(g == 0),
                 stop=(g == PASSES - 1),
             )
-            if g == PASSES - 1:
-                nc.vector.tensor_scalar(out=y[:, cols], in0=acc[e][:, 0:C], scalar1=b_sb[:, e : e + 1], scalar2=None, op0=add)
 
-        for t in range(PACK):
+        nc.vector.tensor_copy(out=rounded[:, 0, :], in_=planes[(1, 0)][:])
+        for t in range(1, PACK):
             nc.gpsimd.tensor_scalar(out=rounded[:, t, :], in0=planes[(1, t)][:], scalar1=1.0, scalar2=0.0, op0=mult, op1=add)
         for t in range(PACK):
-            gather_vector(t, 0)
-            gather_vector(t, 1)
-            gather_scalar(t, 0)
-            gather_scalar(t, 1)
-        interleave(0)
-        interleave(1)
+            for e in range(E):
+                nc.scalar.activation(grouped1[e][:, :, t], rounded[:, t, :].indirect(slots(e)), act.Copy)
+
+        picked_a = held.tile([P, 2, PACK, C], F32, name="picked_a")
         for t in range(PACK):
-            gather_vector(t, 2)
-        interleave(2)
-        multiply(0, 0)
-        multiply(0, 1)
-        for t in range(PACK):
-            gather_vector(t, 3)
-            gather_scalar(t, 2)
-        interleave(3)
-        multiply(0, 2)
-        multiply(1, 0)
-        multiply(1, 1)
-        for t in range(PACK):
-            gather_scalar(t, 3)
-        multiply(0, 3)
-        multiply(1, 2)
-        multiply(1, 3)
+            for e in range(2):
+                nc.vector.tensor_copy(picked_a[:, e, t, :], planes[(0, t)][:].indirect(slots(e)))
+        picked_b = held.tile([P, 2, PACK, C], F32, name="picked_b", tag="late")
+        for e in range(2):
+            for t in range(PACK):
+                nc.vector.tensor_copy(picked_b[:, e, t, :], planes[(0, t)][:].indirect(slots(2 + e)))
+        for e, src in ((0, picked_a[:, 0]), (1, picked_a[:, 1]), (2, picked_b[:, 0])):
+            nc.gpsimd.tensor_scalar(out=grouped0[:, e * C : (e + 1) * C, :], in0=src.rearrange("p t n -> p n t"), scalar1=1.0, scalar2=0.0, op0=mult, op1=add)
+        nc.vector.tensor_copy(out=grouped0[:, 3 * C : 4 * C, :], in_=picked_b[:, 1].rearrange("p t n -> p n t"))
+
+        for first in (0, 2):
+            quantize(0, first, 2, grouped0[:, first * C : (first + 2) * C, :].rearrange("p n t -> p (n t)"))
+            multiply(0, first)
+            multiply(0, first + 1)
+        for e in range(E):
+            quantize(1, e, 1, grouped1[e][:].rearrange("p n t -> p (n t)"))
+            multiply(1, e)
+            nc.vector.tensor_scalar(out=y[:, e * C : (e + 1) * C], in0=acc[e][:, 0:C], scalar1=b_sb[:, e : e + 1], scalar2=None, op0=add)
 
         part1 = held.tile([P, T], F32, name="part1")
         part2 = held.tile([P, T], F32, name="part2")

@@ -17,6 +17,7 @@ P = 128
 PACK = 4
 PASSES = K // (P * PACK)
 OFFS_COLS = C // 16
+SCALAR_SHARE = 192
 
 
 def tile_routed_moe_kernel(tc, xT, w_words, w_scales, b, gate, offs, pos1, pos2, out):
@@ -68,6 +69,9 @@ def tile_routed_moe_kernel(tc, xT, w_words, w_scales, b, gate, offs, pos1, pos2,
         def slots(e):
             return offs_sb[:, e * OFFS_COLS : (e + 1) * OFFS_COLS]
 
+        def round_on_gpsimd(dst, src):
+            nc.gpsimd.tensor_scalar(out=dst, in0=src, scalar1=1.0, scalar2=0.0, op0=mult, op1=add)
+
         def quantize(g, first, count, in_):
             cols = slice(first * C, (first + count) * C)
             nc.vector.quantize_mx(out=x_codes[:, g, cols].bitcast(FP8X4), scales=x_scales[:, g, cols], in_=in_)
@@ -84,9 +88,10 @@ def tile_routed_moe_kernel(tc, xT, w_words, w_scales, b, gate, offs, pos1, pos2,
                 stop=(g == PASSES - 1),
             )
 
-        nc.vector.tensor_copy(out=rounded[:, 0, :], in_=planes[(1, 0)][:])
+        nc.scalar.copy(out=rounded[:, 0, 0:SCALAR_SHARE], in_=planes[(1, 0)][:, 0:SCALAR_SHARE])
+        nc.vector.tensor_copy(out=rounded[:, 0, SCALAR_SHARE:T], in_=planes[(1, 0)][:, SCALAR_SHARE:T])
         for t in range(1, PACK):
-            nc.gpsimd.tensor_scalar(out=rounded[:, t, :], in0=planes[(1, t)][:], scalar1=1.0, scalar2=0.0, op0=mult, op1=add)
+            round_on_gpsimd(rounded[:, t, :], planes[(1, t)][:])
         for t in range(PACK):
             for e in range(E):
                 nc.scalar.activation(grouped1[e][:, :, t], rounded[:, t, :].indirect(slots(e)), act.Copy)
@@ -100,7 +105,7 @@ def tile_routed_moe_kernel(tc, xT, w_words, w_scales, b, gate, offs, pos1, pos2,
             for t in range(PACK):
                 nc.vector.tensor_copy(picked_b[:, e, t, :], planes[(0, t)][:].indirect(slots(2 + e)))
         for e, src in ((0, picked_a[:, 0]), (1, picked_a[:, 1]), (2, picked_b[:, 0])):
-            nc.gpsimd.tensor_scalar(out=grouped0[:, e * C : (e + 1) * C, :], in0=src.rearrange("p t n -> p n t"), scalar1=1.0, scalar2=0.0, op0=mult, op1=add)
+            round_on_gpsimd(grouped0[:, e * C : (e + 1) * C, :], src.rearrange("p t n -> p n t"))
         nc.vector.tensor_copy(out=grouped0[:, 3 * C : 4 * C, :], in_=picked_b[:, 1].rearrange("p t n -> p n t"))
 
         for first in (0, 2):
@@ -110,7 +115,7 @@ def tile_routed_moe_kernel(tc, xT, w_words, w_scales, b, gate, offs, pos1, pos2,
         for e in range(E):
             quantize(1, e, 1, grouped1[e][:].rearrange("p n t -> p (n t)"))
             multiply(1, e)
-            nc.vector.tensor_scalar(out=y[:, e * C : (e + 1) * C], in0=acc[e][:, 0:C], scalar1=b_sb[:, e : e + 1], scalar2=None, op0=add)
+            nc.scalar.activation(out=y[:, e * C : (e + 1) * C], in_=acc[e][:, 0:C], func=act.Identity, bias=b_sb[:, e : e + 1])
 
         part1 = held.tile([P, T], F32, name="part1")
         part2 = held.tile([P, T], F32, name="part2")

@@ -18,6 +18,7 @@ PACK = 4
 PASSES = K // (P * PACK)
 OFFS_COLS = C // 16
 SCALAR_SHARE = 192
+PAD = 16
 
 
 def tile_routed_moe_kernel(tc, xT, w_words, w_scales, b, gate, offs, pos1, pos2, out):
@@ -35,8 +36,10 @@ def tile_routed_moe_kernel(tc, xT, w_words, w_scales, b, gate, offs, pos1, pos2,
         planes = {}
         for t in range(PACK):
             for g in (1, 0):
-                planes[(g, t)] = held.tile([P, T], F32, name="plane%d%d" % (g, t), tag="late" if (g, t) == (1, PACK - 1) else "plane%d%d" % (g, t))
-                nc.sync.dma_start(planes[(g, t)][:], x_planes[g, :, t, :])
+                planes[(g, t)] = held.tile([P, T + PAD * (1 - g)], F32, name="plane%d%d" % (g, t), tag="late" if (g, t) == (1, PACK - 1) else "plane%d%d" % (g, t))
+                if g == 0:
+                    nc.gpsimd.memset(planes[(g, t)][:, T : T + PAD], 0.0)
+                nc.sync.dma_start(planes[(g, t)][:, 0:T], x_planes[g, :, t, :])
 
         w_code_sb = held.tile([P, E * PASSES, N * PACK], U8, name="w_code_sb", align_bytes=64)
         nc.sync.dma_start(w_code_sb[:], w_words.rearrange("e a p n r -> p (e a) (n r)"))
@@ -96,15 +99,14 @@ def tile_routed_moe_kernel(tc, xT, w_words, w_scales, b, gate, offs, pos1, pos2,
             for e in range(E):
                 nc.scalar.activation(grouped1[e][:, :, t], rounded[:, t, :].indirect(slots(e)), act.Copy)
 
-        picked_a = held.tile([P, 2, PACK, C], F32, name="picked_a")
+        picked_a = held.tile([P, PACK, 2 * C], F32, name="picked_a")
         for t in range(PACK):
-            for e in range(2):
-                nc.vector.tensor_copy(picked_a[:, e, t, :], planes[(0, t)][:].indirect(slots(e)))
+            nc.vector.tensor_copy(picked_a[:, t, :], planes[(0, t)][:].indirect(offs_sb[:, 0 : 2 * OFFS_COLS]))
         picked_b = held.tile([P, 2, PACK, C], F32, name="picked_b", tag="late")
         for e in range(2):
             for t in range(PACK):
                 nc.vector.tensor_copy(picked_b[:, e, t, :], planes[(0, t)][:].indirect(slots(2 + e)))
-        for e, src in ((0, picked_a[:, 0]), (1, picked_a[:, 1]), (2, picked_b[:, 0])):
+        for e, src in ((0, picked_a[:, :, 0:C]), (1, picked_a[:, :, C : 2 * C]), (2, picked_b[:, 0])):
             round_on_gpsimd(grouped0[:, e * C : (e + 1) * C, :], src.rearrange("p t n -> p n t"))
         nc.vector.tensor_copy(out=grouped0[:, 3 * C : 4 * C, :], in_=picked_b[:, 1].rearrange("p t n -> p n t"))
 
@@ -115,7 +117,10 @@ def tile_routed_moe_kernel(tc, xT, w_words, w_scales, b, gate, offs, pos1, pos2,
         for e in range(E):
             quantize(1, e, 1, grouped1[e][:].rearrange("p n t -> p (n t)"))
             multiply(1, e)
-            nc.scalar.activation(out=y[:, e * C : (e + 1) * C], in_=acc[e][:, 0:C], func=act.Identity, bias=b_sb[:, e : e + 1])
+            if e < E - 1:
+                nc.scalar.activation(out=y[:, e * C : (e + 1) * C], in_=acc[e][:, 0:C], func=act.Identity, bias=b_sb[:, e : e + 1])
+            else:
+                nc.vector.tensor_scalar(out=y[:, e * C : (e + 1) * C], in0=acc[e][:, 0:C], scalar1=b_sb[:, e : e + 1], scalar2=None, op0=add)
 
         part1 = held.tile([P, T], F32, name="part1")
         part2 = held.tile([P, T], F32, name="part2")

@@ -19,6 +19,7 @@ PASSES = K // (P * PACK)
 OFFS_COLS = C // 16
 SCALAR_SHARE = 192
 PAD = 16
+LAST = 128
 
 
 def tile_routed_moe_kernel(tc, xT, w_words, w_scales, b, gate, offs, pos1, pos2, out):
@@ -126,6 +127,9 @@ def tile_routed_moe_kernel(tc, xT, w_words, w_scales, b, gate, offs, pos1, pos2,
         part2 = held.tile([P, T], F32, name="part2")
         result = held.tile([P, T], F32, name="result")
         nc.vector.tensor_tensor(out=part1[:], in0=y[:].indirect(pos1_sb[:]), in1=gate1_sb[:], op=mult)
-        nc.vector.tensor_tensor(out=part2[:], in0=y[:].indirect(pos2_sb[:]), in1=gate2_sb[:], op=mult)
-        nc.vector.tensor_tensor(out=result[:], in0=part1[:], in1=part2[:], op=add)
-        nc.sync.dma_start(out, result[:])
+        pieces = (slice(0, T - LAST), slice(T - LAST, T))
+        for cols in pieces:
+            nc.vector.tensor_tensor(out=part2[:, cols], in0=y[:].indirect(pos2_sb[:, cols.start // 16 : cols.stop // 16]), in1=gate2_sb[:, cols], op=mult)
+        for cols, queue in zip(pieces, (nc.sync, nc.scalar)):
+            nc.vector.tensor_tensor(out=result[:, cols], in0=part1[:, cols], in1=part2[:, cols], op=add)
+            queue.dma_start(out[:, cols], result[:, cols])

@@ -19,7 +19,9 @@ PASSES = K // (P * PACK)
 OFFS_COLS = C // 16
 SCALAR_SHARE = 192
 PAD = 16
-LAST = 128
+LAST = 256
+H = C // 2
+LOAD_ORDER = ((1, 0), (0, 0), (0, 1), (1, 1), (0, 2), (0, 3), (1, 2), (1, 3))
 
 
 def tile_routed_moe_kernel(tc, xT, w_words, w_scales, b, gate, offs, pos1, pos2, out):
@@ -31,16 +33,17 @@ def tile_routed_moe_kernel(tc, xT, w_words, w_scales, b, gate, offs, pos1, pos2,
         psum = ctx.enter_context(tc.psum_pool(name="psum", bufs=1))
 
         offs_sb = held.tile([P, E * C // 16], U16, name="offs_sb")
-        nc.sync.dma_start(offs_sb[:], offs)
 
         x_planes = xT.rearrange("(g p t) n -> g p t n", p=P, t=PACK)
         planes = {}
-        for t in range(PACK):
-            for g in (1, 0):
+        for g, t in LOAD_ORDER:
+            if True:
                 planes[(g, t)] = held.tile([P, T + PAD * (1 - g)], F32, name="plane%d%d" % (g, t), tag="late" if (g, t) == (1, PACK - 1) else "plane%d%d" % (g, t))
                 if g == 0:
                     nc.gpsimd.memset(planes[(g, t)][:, T : T + PAD], 0.0)
                 nc.sync.dma_start(planes[(g, t)][:, 0:T], x_planes[g, :, t, :])
+                if (g, t) == LOAD_ORDER[0]:
+                    nc.sync.dma_start(offs_sb[:], offs)
 
         w_code_sb = held.tile([P, E * PASSES, N * PACK], U8, name="w_code_sb", align_bytes=64)
         nc.sync.dma_start(w_code_sb[:], w_words.rearrange("e a p n r -> p (e a) (n r)"))
@@ -65,7 +68,7 @@ def tile_routed_moe_kernel(tc, xT, w_words, w_scales, b, gate, offs, pos1, pos2,
         x_codes = held.tile([P, PASSES, E * C], U32, name="x_codes", align_bytes=64)
         x_scales = held.tile([P, PASSES, E * C], U8, name="x_scales", align_bytes=64)
         y = held.tile([P, E * C], F32, name="y")
-        acc = [psum.tile([P, 512], F32, name="acc%d" % e) for e in range(E)]
+        acc = [psum.tile([P, 512], F32, name="acc%d" % e) for e in range(E + 1)]
         rounded = held.tile([P, PACK, T], BF16, name="rounded")
         grouped0 = held.tile([P, E * C, PACK], BF16, name="grouped0", align_bytes=64)
         grouped1 = [held.tile([P, C, PACK], BF16, name="grouped1%d" % e, align_bytes=64) for e in range(E)]
@@ -80,10 +83,10 @@ def tile_routed_moe_kernel(tc, xT, w_words, w_scales, b, gate, offs, pos1, pos2,
             cols = slice(first * C, (first + count) * C)
             nc.vector.quantize_mx(out=x_codes[:, g, cols].bitcast(FP8X4), scales=x_scales[:, g, cols], in_=in_)
 
-        def multiply(g, e):
-            cols = slice(e * C, (e + 1) * C)
+        def multiply(g, e, bank=None, first=0, count=C):
+            cols = slice(e * C + first, e * C + first + count)
             nc.tensor.matmul_mx(
-                out=acc[e][:, 0:C],
+                out=acc[e if bank is None else bank][:, 0:count],
                 lhsT=w_code_sb[:, e * PASSES + g, :].bitcast(FP8X4),
                 lhsT_scale=w_scale_sb[:, e * PASSES + g, :],
                 rhs=x_codes[:, g, cols].bitcast(FP8X4),
@@ -98,7 +101,14 @@ def tile_routed_moe_kernel(tc, xT, w_words, w_scales, b, gate, offs, pos1, pos2,
             round_on_gpsimd(rounded[:, t, :], planes[(1, t)][:])
         for t in range(PACK):
             for e in range(E):
-                nc.scalar.activation(grouped1[e][:, :, t], rounded[:, t, :].indirect(slots(e)), act.Copy)
+                if (e, t) != (E - 1, PACK - 1):
+                    nc.scalar.activation(grouped1[e][:, :, t], rounded[:, t, :].indirect(slots(e)), act.Copy)
+        for h in range(2):
+            nc.scalar.activation(
+                grouped1[E - 1][:, h * H : (h + 1) * H, PACK - 1],
+                rounded[:, PACK - 1, :].indirect(offs_sb[:, (E - 1) * OFFS_COLS + h * H // 16 : (E - 1) * OFFS_COLS + (h + 1) * H // 16]),
+                act.Copy,
+            )
 
         picked_a = held.tile([P, PACK, 2 * C], F32, name="picked_a")
         for t in range(PACK):
@@ -114,14 +124,28 @@ def tile_routed_moe_kernel(tc, xT, w_words, w_scales, b, gate, offs, pos1, pos2,
         for first in (0, 2):
             quantize(0, first, 2, grouped0[:, first * C : (first + 2) * C, :].rearrange("p n t -> p (n t)"))
             multiply(0, first)
-            multiply(0, first + 1)
-        for e in range(E):
+            if first == 0:
+                multiply(0, 1)
+            else:
+                for h in range(2):
+                    multiply(0, E - 1, bank=E - 1 + h, first=h * H, count=H)
+        for e in range(E - 1):
             quantize(1, e, 1, grouped1[e][:].rearrange("p n t -> p (n t)"))
             multiply(1, e)
-            if e < E - 1:
-                nc.scalar.activation(out=y[:, e * C : (e + 1) * C], in_=acc[e][:, 0:C], func=act.Identity, bias=b_sb[:, e : e + 1])
+            nc.scalar.activation(out=y[:, e * C : (e + 1) * C], in_=acc[e][:, 0:C], func=act.Identity, bias=b_sb[:, e : e + 1])
+        e = E - 1
+        for h in range(2):
+            nc.vector.quantize_mx(
+                out=x_codes[:, 1, e * C + h * H : e * C + (h + 1) * H].bitcast(FP8X4),
+                scales=x_scales[:, 1, e * C + h * H : e * C + (h + 1) * H],
+                in_=grouped1[e][:, h * H : (h + 1) * H, :].rearrange("p n t -> p (n t)"),
+            )
+            multiply(1, e, bank=e + h, first=h * H, count=H)
+            dst = y[:, e * C + h * H : e * C + (h + 1) * H]
+            if h == 1:
+                nc.scalar.activation(out=dst, in_=acc[e + h][:, 0:H], func=act.Identity, bias=b_sb[:, e : e + 1])
             else:
-                nc.vector.tensor_scalar(out=y[:, e * C : (e + 1) * C], in0=acc[e][:, 0:C], scalar1=b_sb[:, e : e + 1], scalar2=None, op0=add)
+                nc.vector.tensor_scalar(out=dst, in0=acc[e + h][:, 0:H], scalar1=b_sb[:, e : e + 1], scalar2=None, op0=add)
 
         part1 = held.tile([P, T], F32, name="part1")
         part2 = held.tile([P, T], F32, name="part2")

@@ -17,11 +17,13 @@ P = 128
 PACK = 4
 PASSES = K // (P * PACK)
 OFFS_COLS = C // 16
-SCALAR_SHARE = 192
+SCALAR_SHARE = 256
 PAD = 16
 LAST = 256
 H = C // 2
-LOAD_ORDER = ((1, 0), (0, 0), (0, 1), (1, 1), (0, 2), (0, 3), (1, 2), (1, 3))
+LOAD_ORDER = ((1, 0), (0, 0), (1, 1), (0, 1), (1, 2), (0, 2), (1, 3), (0, 3))
+SCALAR_UNITS = ((1, 0), (1, 1), (1, 2), (1, 3), (0, 3))
+PAIR_SLOT = {(1, 3): "plane00", (0, 3): "plane01"}
 
 
 def tile_routed_moe_kernel(tc, xT, w_words, w_scales, b, gate, offs, pos1, pos2, out):
@@ -38,12 +40,15 @@ def tile_routed_moe_kernel(tc, xT, w_words, w_scales, b, gate, offs, pos1, pos2,
         planes = {}
         for g, t in LOAD_ORDER:
             if True:
-                planes[(g, t)] = held.tile([P, T + PAD * (1 - g)], F32, name="plane%d%d" % (g, t), tag="late" if (g, t) == (1, PACK - 1) else "plane%d%d" % (g, t))
+                planes[(g, t)] = held.tile([P, T + PAD * (1 - g)], F32, name="plane%d%d" % (g, t), tag="late" if (g, t) == (1, PACK - 1) else "plane%d%d" % (g, t), align_bytes=64)
                 if g == 0:
                     nc.gpsimd.memset(planes[(g, t)][:, T : T + PAD], 0.0)
-                nc.sync.dma_start(planes[(g, t)][:, 0:T], x_planes[g, :, t, :])
                 if (g, t) == LOAD_ORDER[0]:
+                    nc.sync.dma_start(planes[(g, t)][:, 0:SCALAR_SHARE], x_planes[g, :, t, 0:SCALAR_SHARE])
+                    nc.sync.dma_start(planes[(g, t)][:, SCALAR_SHARE:T], x_planes[g, :, t, SCALAR_SHARE:T])
                     nc.sync.dma_start(offs_sb[:], offs)
+                else:
+                    nc.sync.dma_start(planes[(g, t)][:, 0:T], x_planes[g, :, t, :])
 
         w_code_sb = held.tile([P, E * PASSES, N * PACK], U8, name="w_code_sb", align_bytes=64)
         nc.sync.dma_start(w_code_sb[:], w_words.rearrange("e a p n r -> p (e a) (n r)"))
@@ -69,9 +74,7 @@ def tile_routed_moe_kernel(tc, xT, w_words, w_scales, b, gate, offs, pos1, pos2,
         x_scales = held.tile([P, PASSES, E * C], U8, name="x_scales", align_bytes=64)
         y = held.tile([P, E * C], F32, name="y")
         acc = [psum.tile([P, 512], F32, name="acc%d" % e) for e in range(E + 1)]
-        rounded = held.tile([P, PACK, T], BF16, name="rounded")
-        grouped0 = held.tile([P, E * C, PACK], BF16, name="grouped0", align_bytes=64)
-        grouped1 = [held.tile([P, C, PACK], BF16, name="grouped1%d" % e, align_bytes=64) for e in range(E)]
+        rounded = [held.tile([P, PACK, T], BF16, name="rounded%d" % g) for g in range(PASSES)]
 
         def slots(e):
             return offs_sb[:, e * OFFS_COLS : (e + 1) * OFFS_COLS]
@@ -83,7 +86,7 @@ def tile_routed_moe_kernel(tc, xT, w_words, w_scales, b, gate, offs, pos1, pos2,
             cols = slice(first * C, (first + count) * C)
             nc.vector.quantize_mx(out=x_codes[:, g, cols].bitcast(FP8X4), scales=x_scales[:, g, cols], in_=in_)
 
-        def multiply(g, e, bank=None, first=0, count=C):
+        def multiply(g, e, start, stop, bank=None, first=0, count=C):
             cols = slice(e * C + first, e * C + first + count)
             nc.tensor.matmul_mx(
                 out=acc[e if bank is None else bank][:, 0:count],
@@ -91,61 +94,97 @@ def tile_routed_moe_kernel(tc, xT, w_words, w_scales, b, gate, offs, pos1, pos2,
                 lhsT_scale=w_scale_sb[:, e * PASSES + g, :],
                 rhs=x_codes[:, g, cols].bitcast(FP8X4),
                 rhs_scale=x_scales[:, g, cols],
-                start=(g == 0),
-                stop=(g == PASSES - 1),
+                start=start,
+                stop=stop,
             )
 
-        nc.scalar.copy(out=rounded[:, 0, 0:SCALAR_SHARE], in_=planes[(1, 0)][:, 0:SCALAR_SHARE])
-        nc.vector.tensor_copy(out=rounded[:, 0, SCALAR_SHARE:T], in_=planes[(1, 0)][:, SCALAR_SHARE:T])
-        for t in range(1, PACK):
-            round_on_gpsimd(rounded[:, t, :], planes[(1, t)][:])
-        for t in range(PACK):
-            for e in range(E):
-                if (e, t) != (E - 1, PACK - 1):
-                    nc.scalar.activation(grouped1[e][:, :, t], rounded[:, t, :].indirect(slots(e)), act.Copy)
-        for h in range(2):
-            nc.scalar.activation(
-                grouped1[E - 1][:, h * H : (h + 1) * H, PACK - 1],
-                rounded[:, PACK - 1, :].indirect(offs_sb[:, (E - 1) * OFFS_COLS + h * H // 16 : (E - 1) * OFFS_COLS + (h + 1) * H // 16]),
-                act.Copy,
-            )
+        nc.scalar.copy(out=rounded[1][:, 0, 0:SCALAR_SHARE], in_=planes[(1, 0)][:, 0:SCALAR_SHARE])
+        nc.vector.tensor_copy(out=rounded[1][:, 0, SCALAR_SHARE:T], in_=planes[(1, 0)][:, SCALAR_SHARE:T])
+        for g, t in LOAD_ORDER[1:]:
+            round_on_gpsimd(rounded[g][:, t, :], planes[(g, t)][:, 0:T])
 
-        picked_a = held.tile([P, PACK, 2 * C], F32, name="picked_a")
+        picked_a = held.tile([P, PACK, 2 * C], F32, name="picked_a", align_bytes=64)
         for t in range(PACK):
             nc.vector.tensor_copy(picked_a[:, t, :], planes[(0, t)][:].indirect(offs_sb[:, 0 : 2 * OFFS_COLS]))
-        picked_b = held.tile([P, 2, PACK, C], F32, name="picked_b", tag="late")
+        grouped_a = held.tile([P, 2 * C, PACK], BF16, name="grouped_a", align_bytes=64)
         for e in range(2):
-            for t in range(PACK):
-                nc.vector.tensor_copy(picked_b[:, e, t, :], planes[(0, t)][:].indirect(slots(2 + e)))
-        for e, src in ((0, picked_a[:, :, 0:C]), (1, picked_a[:, :, C : 2 * C]), (2, picked_b[:, 0])):
-            round_on_gpsimd(grouped0[:, e * C : (e + 1) * C, :], src.rearrange("p t n -> p n t"))
-        nc.vector.tensor_copy(out=grouped0[:, 3 * C : 4 * C, :], in_=picked_b[:, 1].rearrange("p t n -> p n t"))
+            round_on_gpsimd(grouped_a[:, e * C : (e + 1) * C, :], picked_a[:, :, e * C : (e + 1) * C].rearrange("p t n -> p n t"))
+        picked_b = held.tile([P, PACK, C], F32, name="picked_b", tag="late", align_bytes=64)
+        for t in range(PACK):
+            nc.vector.tensor_copy(picked_b[:, t, :], planes[(0, t)][:].indirect(slots(2)))
+        grouped_b = held.tile([P, C, PACK], BF16, name="grouped_b", align_bytes=64)
+        nc.vector.tensor_copy(out=grouped_b[:], in_=picked_b[:].rearrange("p t n -> p n t"))
 
-        for first in (0, 2):
-            quantize(0, first, 2, grouped0[:, first * C : (first + 2) * C, :].rearrange("p n t -> p (n t)"))
-            multiply(0, first)
-            if first == 0:
-                multiply(0, 1)
+        pair_tiles = {}
+        pairs01 = held.tile([P, 2, 2, C, 2], BF16, name="pairs01", align_bytes=64)
+        for g, e in SCALAR_UNITS:
+            if e < 2:
+                pairs = pairs01[:, e]
+            else:
+                pairs = held.tile([P, 2, C, 2], BF16, name="pairs%d%d" % (g, e), tag=PAIR_SLOT.get((g, e), "pairs%d%d" % (g, e)), align_bytes=64)
+            pair_tiles[(g, e)] = pairs
+            for t in range(PACK):
+                if (g, e) == SCALAR_UNITS[-1] and t == PACK - 1:
+                    for h in range(2):
+                        nc.scalar.activation(
+                            pairs[:, t // 2, h * H : (h + 1) * H, t % 2],
+                            rounded[g][:, t, :].indirect(offs_sb[:, e * OFFS_COLS + h * H // 16 : e * OFFS_COLS + (h + 1) * H // 16]),
+                            act.Copy,
+                        )
+                else:
+                    nc.scalar.activation(pairs[:, t // 2, :, t % 2], rounded[g][:, t, :].indirect(slots(e)), act.Copy)
+
+        def merge(dst, unit):
+            nc.vector.tensor_copy(
+                out=dst.rearrange("p n t -> p (n t)").bitcast(F32).rearrange("p (n u) -> p n u", u=2),
+                in_=pair_tiles[unit][:].rearrange("p u n i -> p (u n i)").bitcast(F32).rearrange("p (u n) -> p n u", u=2),
+            )
+
+        def read_bank(e):
+            nc.scalar.activation(out=y[:, e * C : (e + 1) * C], in_=acc[e][:, 0:C], func=act.Identity, bias=b_sb[:, e : e + 1])
+
+        merged01 = held.tile([P, 2 * C, PACK], BF16, name="merged01", tag="late", align_bytes=64)
+        nc.vector.tensor_copy(
+            out=merged01[:].rearrange("p n t -> p (n t)").bitcast(F32).rearrange("p (a n u) -> p a n u", a=2, u=2),
+            in_=pairs01[:].rearrange("p a u n i -> p (a u n i)").bitcast(F32).rearrange("p (a u n) -> p a n u", a=2, u=2),
+        )
+        quantize(0, 0, 2, grouped_a[:].rearrange("p n t -> p (n t)"))
+        multiply(0, 0, True, False)
+        multiply(0, 1, True, False)
+        quantize(0, 2, 1, grouped_b[:].rearrange("p n t -> p (n t)"))
+        multiply(0, 2, True, False)
+        quantize(1, 0, 2, merged01[:].rearrange("p n t -> p (n t)"))
+        for e in range(2):
+            multiply(1, e, False, True)
+            read_bank(e)
+        for (g, e), slot in zip(SCALAR_UNITS[2:], ("picked_a", "grouped_a", "grouped_b")):
+            merged = held.tile([P, C, PACK], BF16, name="merged%d%d" % (g, e), tag=slot, align_bytes=64)
+            if e < E - 1:
+                merge(merged[:], (g, e))
+                quantize(g, e, 1, merged[:].rearrange("p n t -> p (n t)"))
+                multiply(g, e, False, True)
+                read_bank(e)
+            elif g == 1:
+                merge(merged[:], (g, e))
+                quantize(g, e, 1, merged[:].rearrange("p n t -> p (n t)"))
+                for h in range(2):
+                    multiply(g, e, True, False, bank=e + h, first=h * H, count=H)
             else:
                 for h in range(2):
-                    multiply(0, E - 1, bank=E - 1 + h, first=h * H, count=H)
-        for e in range(E - 1):
-            quantize(1, e, 1, grouped1[e][:].rearrange("p n t -> p (n t)"))
-            multiply(1, e)
-            nc.scalar.activation(out=y[:, e * C : (e + 1) * C], in_=acc[e][:, 0:C], func=act.Identity, bias=b_sb[:, e : e + 1])
-        e = E - 1
-        for h in range(2):
-            nc.vector.quantize_mx(
-                out=x_codes[:, 1, e * C + h * H : e * C + (h + 1) * H].bitcast(FP8X4),
-                scales=x_scales[:, 1, e * C + h * H : e * C + (h + 1) * H],
-                in_=grouped1[e][:, h * H : (h + 1) * H, :].rearrange("p n t -> p (n t)"),
-            )
-            multiply(1, e, bank=e + h, first=h * H, count=H)
-            dst = y[:, e * C + h * H : e * C + (h + 1) * H]
-            if h == 1:
-                nc.scalar.activation(out=dst, in_=acc[e + h][:, 0:H], func=act.Identity, bias=b_sb[:, e : e + 1])
-            else:
-                nc.vector.tensor_scalar(out=dst, in0=acc[e + h][:, 0:H], scalar1=b_sb[:, e : e + 1], scalar2=None, op0=add)
+                    part = slice(h * H, (h + 1) * H)
+                    nc.vector.tensor_copy(
+                        out=merged[:, part, :].rearrange("p n t -> p (n t)").bitcast(F32).rearrange("p (n u) -> p n u", u=2),
+                        in_=pair_tiles[(g, e)][:, :, part, :].rearrange("p u n i -> p u (n i)").bitcast(F32).rearrange("p u n -> p n u"),
+                    )
+                for h in range(2):
+                    part = slice(h * H, (h + 1) * H)
+                    nc.vector.quantize_mx(
+                        out=x_codes[:, g, e * C + h * H : e * C + (h + 1) * H].bitcast(FP8X4),
+                        scales=x_scales[:, g, e * C + h * H : e * C + (h + 1) * H],
+                        in_=merged[:, part, :].rearrange("p n t -> p (n t)"),
+                    )
+                    multiply(g, e, False, True, bank=e + h, first=h * H, count=H)
+                    nc.scalar.activation(out=y[:, e * C + h * H : e * C + (h + 1) * H], in_=acc[e + h][:, 0:H], func=act.Identity, bias=b_sb[:, e : e + 1])
 
         part1 = held.tile([P, T], F32, name="part1")
         part2 = held.tile([P, T], F32, name="part2")

@@ -21,6 +21,7 @@ SCALAR_SHARE = 256
 PAD = 16
 LAST = 256
 H = C // 2
+FIRST = 448
 LOAD_ORDER = ((1, 0), (0, 0), (1, 1), (0, 1), (1, 2), (0, 2), (1, 3), (0, 3))
 SCALAR_UNITS = ((1, 0), (1, 1), (1, 2), (1, 3), (0, 3))
 PAIR_SLOT = {(1, 3): "plane00", (0, 3): "plane01"}
@@ -103,17 +104,18 @@ def tile_routed_moe_kernel(tc, xT, w_words, w_scales, b, gate, offs, pos1, pos2,
         for g, t in LOAD_ORDER[1:]:
             round_on_gpsimd(rounded[g][:, t, :], planes[(g, t)][:, 0:T])
 
-        picked_a = held.tile([P, PACK, 2 * C], F32, name="picked_a", align_bytes=64)
+        picked_a = held.tile([P, PACK, FIRST], F32, name="picked_a", align_bytes=64)
         for t in range(PACK):
-            nc.vector.tensor_copy(picked_a[:, t, :], planes[(0, t)][:].indirect(offs_sb[:, 0 : 2 * OFFS_COLS]))
+            nc.vector.tensor_copy(picked_a[:, t, :], planes[(0, t)][:].indirect(offs_sb[:, 0 : FIRST // 16]))
         grouped_a = held.tile([P, 2 * C, PACK], BF16, name="grouped_a", align_bytes=64)
-        for e in range(2):
-            round_on_gpsimd(grouped_a[:, e * C : (e + 1) * C, :], picked_a[:, :, e * C : (e + 1) * C].rearrange("p t n -> p n t"))
-        picked_b = held.tile([P, PACK, C], F32, name="picked_b", tag="late", align_bytes=64)
+        for cols in (slice(0, C), slice(C, FIRST)):
+            round_on_gpsimd(grouped_a[:, cols, :], picked_a[:, :, cols].rearrange("p t n -> p n t"))
+        picked_b = held.tile([P, PACK, 3 * C - FIRST], F32, name="picked_b", tag="late", align_bytes=64)
         for t in range(PACK):
-            nc.vector.tensor_copy(picked_b[:, t, :], planes[(0, t)][:].indirect(slots(2)))
+            nc.vector.tensor_copy(picked_b[:, t, :], planes[(0, t)][:].indirect(offs_sb[:, FIRST // 16 : 3 * OFFS_COLS]))
         grouped_b = held.tile([P, C, PACK], BF16, name="grouped_b", align_bytes=64)
-        nc.vector.tensor_copy(out=grouped_b[:], in_=picked_b[:].rearrange("p t n -> p n t"))
+        nc.vector.tensor_copy(out=grouped_a[:, FIRST : 2 * C, :], in_=picked_b[:, :, 0 : 2 * C - FIRST].rearrange("p t n -> p n t"))
+        nc.vector.tensor_copy(out=grouped_b[:], in_=picked_b[:, :, 2 * C - FIRST : 3 * C - FIRST].rearrange("p t n -> p n t"))
 
         pair_tiles = {}
         pairs01 = held.tile([P, 2, 2, C, 2], BF16, name="pairs01", align_bytes=64)

@@ -18,13 +18,10 @@ PACK = 4
 PASSES = K // (P * PACK)
 OFFS_COLS = C // 16
 SCALAR_SHARE = 256
-PAD = 16
 LAST = 256
 H = C // 2
-FIRST = 448
 LOAD_ORDER = ((1, 0), (0, 0), (1, 1), (0, 1), (1, 2), (0, 2), (1, 3), (0, 3))
-SCALAR_UNITS = ((1, 0), (1, 1), (1, 2), (1, 3), (0, 3))
-PAIR_SLOT = {(1, 3): "plane00", (0, 3): "plane01"}
+EARLY = 128
 
 
 def tile_routed_moe_kernel(tc, xT, w_words, w_scales, b, gate, offs, pos1, pos2, out):
@@ -40,16 +37,13 @@ def tile_routed_moe_kernel(tc, xT, w_words, w_scales, b, gate, offs, pos1, pos2,
         x_planes = xT.rearrange("(g p t) n -> g p t n", p=P, t=PACK)
         planes = {}
         for g, t in LOAD_ORDER:
-            if True:
-                planes[(g, t)] = held.tile([P, T + PAD * (1 - g)], F32, name="plane%d%d" % (g, t), tag="late" if (g, t) == (1, PACK - 1) else "plane%d%d" % (g, t), align_bytes=64)
-                if g == 0:
-                    nc.gpsimd.memset(planes[(g, t)][:, T : T + PAD], 0.0)
-                if (g, t) == LOAD_ORDER[0]:
-                    nc.sync.dma_start(planes[(g, t)][:, 0:SCALAR_SHARE], x_planes[g, :, t, 0:SCALAR_SHARE])
-                    nc.sync.dma_start(planes[(g, t)][:, SCALAR_SHARE:T], x_planes[g, :, t, SCALAR_SHARE:T])
-                    nc.sync.dma_start(offs_sb[:], offs)
-                else:
-                    nc.sync.dma_start(planes[(g, t)][:, 0:T], x_planes[g, :, t, :])
+            planes[(g, t)] = held.tile([P, T], F32, name="plane%d%d" % (g, t), tag="late" if (g, t) == (1, PACK - 1) else "plane%d%d" % (g, t), align_bytes=64)
+            if (g, t) == LOAD_ORDER[0]:
+                nc.sync.dma_start(planes[(g, t)][:, 0:SCALAR_SHARE], x_planes[g, :, t, 0:SCALAR_SHARE])
+                nc.sync.dma_start(planes[(g, t)][:, SCALAR_SHARE:T], x_planes[g, :, t, SCALAR_SHARE:T])
+                nc.sync.dma_start(offs_sb[:], offs)
+            else:
+                nc.sync.dma_start(planes[(g, t)][:], x_planes[g, :, t, :])
 
         w_code_sb = held.tile([P, E * PASSES, N * PACK], U8, name="w_code_sb", align_bytes=64)
         nc.sync.dma_start(w_code_sb[:], w_words.rearrange("e a p n r -> p (e a) (n r)"))
@@ -75,7 +69,8 @@ def tile_routed_moe_kernel(tc, xT, w_words, w_scales, b, gate, offs, pos1, pos2,
         x_scales = held.tile([P, PASSES, E * C], U8, name="x_scales", align_bytes=64)
         y = held.tile([P, E * C], F32, name="y")
         acc = [psum.tile([P, 512], F32, name="acc%d" % e) for e in range(E + 1)]
-        rounded = [held.tile([P, PACK, T], BF16, name="rounded%d" % g) for g in range(PASSES)]
+        rounded1 = held.tile([P, PACK, T], BF16, name="rounded1")
+        rounded0 = held.tile([P, 2, T], BF16, name="rounded0")
 
         def slots(e):
             return offs_sb[:, e * OFFS_COLS : (e + 1) * OFFS_COLS]
@@ -99,94 +94,102 @@ def tile_routed_moe_kernel(tc, xT, w_words, w_scales, b, gate, offs, pos1, pos2,
                 stop=stop,
             )
 
-        nc.scalar.copy(out=rounded[1][:, 0, 0:SCALAR_SHARE], in_=planes[(1, 0)][:, 0:SCALAR_SHARE])
-        nc.vector.tensor_copy(out=rounded[1][:, 0, SCALAR_SHARE:T], in_=planes[(1, 0)][:, SCALAR_SHARE:T])
+        nc.scalar.copy(out=rounded1[:, 0, 0:SCALAR_SHARE], in_=planes[(1, 0)][:, 0:SCALAR_SHARE])
+        nc.vector.tensor_copy(out=rounded1[:, 0, SCALAR_SHARE:T], in_=planes[(1, 0)][:, SCALAR_SHARE:T])
         for g, t in LOAD_ORDER[1:]:
-            round_on_gpsimd(rounded[g][:, t, :], planes[(g, t)][:, 0:T])
+            if g == 1:
+                round_on_gpsimd(rounded1[:, t, :], planes[(g, t)][:])
+            elif t >= 2:
+                round_on_gpsimd(rounded0[:, t - 2, :], planes[(g, t)][:])
 
-        picked_a = held.tile([P, PACK, FIRST], F32, name="picked_a", align_bytes=64)
+        pairs12 = held.tile([P, 2, C, 2], BF16, name="pairs12", align_bytes=64)
+        for t in range(2):
+            nc.vector.tensor_copy(pairs12[:, 0, 0:EARLY, t], planes[(1, t)][:].indirect(offs_sb[:, 2 * OFFS_COLS : 2 * OFFS_COLS + EARLY // 16]))
+
+        picked = [held.tile([P, PACK, C], F32, name="picked%d" % e, align_bytes=64) for e in range(2)]
         for t in range(PACK):
-            nc.vector.tensor_copy(picked_a[:, t, :], planes[(0, t)][:].indirect(offs_sb[:, 0 : FIRST // 16]))
+            for e in range(2):
+                nc.vector.tensor_copy(picked[e][:, t, :], planes[(0, t)][:].indirect(slots(e)))
         grouped_a = held.tile([P, 2 * C, PACK], BF16, name="grouped_a", align_bytes=64)
-        for cols in (slice(0, C), slice(C, FIRST)):
-            round_on_gpsimd(grouped_a[:, cols, :], picked_a[:, :, cols].rearrange("p t n -> p n t"))
-        picked_b = held.tile([P, PACK, 3 * C - FIRST], F32, name="picked_b", tag="late", align_bytes=64)
-        for t in range(PACK):
-            nc.vector.tensor_copy(picked_b[:, t, :], planes[(0, t)][:].indirect(offs_sb[:, FIRST // 16 : 3 * OFFS_COLS]))
-        grouped_b = held.tile([P, C, PACK], BF16, name="grouped_b", align_bytes=64)
-        nc.vector.tensor_copy(out=grouped_a[:, FIRST : 2 * C, :], in_=picked_b[:, :, 0 : 2 * C - FIRST].rearrange("p t n -> p n t"))
-        nc.vector.tensor_copy(out=grouped_b[:], in_=picked_b[:, :, 2 * C - FIRST : 3 * C - FIRST].rearrange("p t n -> p n t"))
+        for e in range(2):
+            round_on_gpsimd(grouped_a[:, e * C : (e + 1) * C, :], picked[e][:].rearrange("p t n -> p n t"))
 
-        pair_tiles = {}
+        pairs0 = held.tile([P, 2, 2, C, 2], BF16, name="pairs0", tag="late", align_bytes=64)
+        for e in (2, 3):
+            for t in range(2):
+                nc.vector.tensor_copy(pairs0[:, e - 2, 0, :, t], planes[(0, t)][:].indirect(slots(e)))
+
         pairs01 = held.tile([P, 2, 2, C, 2], BF16, name="pairs01", align_bytes=64)
-        for g, e in SCALAR_UNITS:
-            if e < 2:
-                pairs = pairs01[:, e]
-            else:
-                pairs = held.tile([P, 2, C, 2], BF16, name="pairs%d%d" % (g, e), tag=PAIR_SLOT.get((g, e), "pairs%d%d" % (g, e)), align_bytes=64)
-            pair_tiles[(g, e)] = pairs
+        for e in range(3):
+            pairs = pairs01[:, e] if e < 2 else pairs12[:]
             for t in range(PACK):
-                if (g, e) == SCALAR_UNITS[-1] and t == PACK - 1:
-                    for h in range(2):
-                        nc.scalar.activation(
-                            pairs[:, t // 2, h * H : (h + 1) * H, t % 2],
-                            rounded[g][:, t, :].indirect(offs_sb[:, e * OFFS_COLS + h * H // 16 : e * OFFS_COLS + (h + 1) * H // 16]),
-                            act.Copy,
-                        )
+                if e == 2 and t < 2:
+                    nc.scalar.activation(pairs[:, 0, EARLY:C, t], rounded1[:, t, :].indirect(offs_sb[:, 2 * OFFS_COLS + EARLY // 16 : 3 * OFFS_COLS]), act.Copy)
                 else:
-                    nc.scalar.activation(pairs[:, t // 2, :, t % 2], rounded[g][:, t, :].indirect(slots(e)), act.Copy)
+                    nc.scalar.activation(pairs[:, t // 2, :, t % 2], rounded1[:, t, :].indirect(slots(e)), act.Copy)
+        for e in (2, 3):
+            for t in range(2):
+                nc.scalar.activation(pairs0[:, e - 2, 1, :, t], rounded0[:, t, :].indirect(slots(e)), act.Copy)
+        pairs13 = held.tile([P, 2, C, 2], BF16, name="pairs13", tag="plane00", align_bytes=64)
+        for t in range(PACK):
+            if t == PACK - 1:
+                for h in range(2):
+                    nc.scalar.activation(
+                        pairs13[:, t // 2, h * H : (h + 1) * H, t % 2],
+                        rounded1[:, t, :].indirect(offs_sb[:, 3 * OFFS_COLS + h * H // 16 : 3 * OFFS_COLS + (h + 1) * H // 16]),
+                        act.Copy,
+                    )
+            else:
+                nc.scalar.activation(pairs13[:, t // 2, :, t % 2], rounded1[:, t, :].indirect(slots(3)), act.Copy)
 
-        def merge(dst, unit):
+        def merge_two(dst, src):
             nc.vector.tensor_copy(
-                out=dst.rearrange("p n t -> p (n t)").bitcast(F32).rearrange("p (n u) -> p n u", u=2),
-                in_=pair_tiles[unit][:].rearrange("p u n i -> p (u n i)").bitcast(F32).rearrange("p (u n) -> p n u", u=2),
+                out=dst.rearrange("p n t -> p (n t)").bitcast(F32).rearrange("p (a n u) -> p a n u", a=2, u=2),
+                in_=src.rearrange("p a u n i -> p (a u n i)").bitcast(F32).rearrange("p (a u n) -> p a n u", a=2, u=2),
             )
 
         def read_bank(e):
             nc.scalar.activation(out=y[:, e * C : (e + 1) * C], in_=acc[e][:, 0:C], func=act.Identity, bias=b_sb[:, e : e + 1])
 
-        merged01 = held.tile([P, 2 * C, PACK], BF16, name="merged01", tag="late", align_bytes=64)
-        nc.vector.tensor_copy(
-            out=merged01[:].rearrange("p n t -> p (n t)").bitcast(F32).rearrange("p (a n u) -> p a n u", a=2, u=2),
-            in_=pairs01[:].rearrange("p a u n i -> p (a u n i)").bitcast(F32).rearrange("p (a u n) -> p a n u", a=2, u=2),
-        )
         quantize(0, 0, 2, grouped_a[:].rearrange("p n t -> p (n t)"))
         multiply(0, 0, True, False)
         multiply(0, 1, True, False)
-        quantize(0, 2, 1, grouped_b[:].rearrange("p n t -> p (n t)"))
-        multiply(0, 2, True, False)
+        merged01 = held.tile([P, 2 * C, PACK], BF16, name="merged01", tag="picked1", align_bytes=64)
+        merge_two(merged01[:], pairs01[:])
         quantize(1, 0, 2, merged01[:].rearrange("p n t -> p (n t)"))
         for e in range(2):
             multiply(1, e, False, True)
             read_bank(e)
-        for (g, e), slot in zip(SCALAR_UNITS[2:], ("picked_a", "grouped_a", "grouped_b")):
-            merged = held.tile([P, C, PACK], BF16, name="merged%d%d" % (g, e), tag=slot, align_bytes=64)
-            if e < E - 1:
-                merge(merged[:], (g, e))
-                quantize(g, e, 1, merged[:].rearrange("p n t -> p (n t)"))
-                multiply(g, e, False, True)
-                read_bank(e)
-            elif g == 1:
-                merge(merged[:], (g, e))
-                quantize(g, e, 1, merged[:].rearrange("p n t -> p (n t)"))
-                for h in range(2):
-                    multiply(g, e, True, False, bank=e + h, first=h * H, count=H)
-            else:
-                for h in range(2):
-                    part = slice(h * H, (h + 1) * H)
-                    nc.vector.tensor_copy(
-                        out=merged[:, part, :].rearrange("p n t -> p (n t)").bitcast(F32).rearrange("p (n u) -> p n u", u=2),
-                        in_=pair_tiles[(g, e)][:, :, part, :].rearrange("p u n i -> p u (n i)").bitcast(F32).rearrange("p u n -> p n u"),
-                    )
-                for h in range(2):
-                    part = slice(h * H, (h + 1) * H)
-                    nc.vector.quantize_mx(
-                        out=x_codes[:, g, e * C + h * H : e * C + (h + 1) * H].bitcast(FP8X4),
-                        scales=x_scales[:, g, e * C + h * H : e * C + (h + 1) * H],
-                        in_=merged[:, part, :].rearrange("p n t -> p (n t)"),
-                    )
-                    multiply(g, e, False, True, bank=e + h, first=h * H, count=H)
-                    nc.scalar.activation(out=y[:, e * C + h * H : e * C + (h + 1) * H], in_=acc[e + h][:, 0:H], func=act.Identity, bias=b_sb[:, e : e + 1])
+        merged12 = held.tile([P, C, PACK], BF16, name="merged12", tag="picked0", align_bytes=64)
+        nc.vector.tensor_copy(
+            out=merged12[:].rearrange("p n t -> p (n t)").bitcast(F32).rearrange("p (n u) -> p n u", u=2),
+            in_=pairs12[:].rearrange("p u n i -> p (u n i)").bitcast(F32).rearrange("p (u n) -> p n u", u=2),
+        )
+        quantize(1, 2, 1, merged12[:].rearrange("p n t -> p (n t)"))
+        multiply(1, 2, True, False)
+        merged023 = held.tile([P, 2 * C, PACK], BF16, name="merged023", tag="grouped_a", align_bytes=64)
+        merge_two(merged023[:], pairs0[:])
+        quantize(0, 2, 2, merged023[:].rearrange("p n t -> p (n t)"))
+        multiply(0, 2, False, True)
+        read_bank(2)
+        for h in range(2):
+            multiply(0, 3, True, False, bank=3 + h, first=h * H, count=H)
+        merged13 = held.tile([P, C, PACK], BF16, name="merged13", tag="picked1", align_bytes=64)
+        for h in range(2):
+            part = slice(h * H, (h + 1) * H)
+            nc.vector.tensor_copy(
+                out=merged13[:, part, :].rearrange("p n t -> p (n t)").bitcast(F32).rearrange("p (n u) -> p n u", u=2),
+                in_=pairs13[:, :, part, :].rearrange("p u n i -> p u (n i)").bitcast(F32).rearrange("p u n -> p n u"),
+            )
+        for h in range(2):
+            part = slice(h * H, (h + 1) * H)
+            nc.vector.quantize_mx(
+                out=x_codes[:, 1, 3 * C + h * H : 3 * C + (h + 1) * H].bitcast(FP8X4),
+                scales=x_scales[:, 1, 3 * C + h * H : 3 * C + (h + 1) * H],
+                in_=merged13[:, part, :].rearrange("p n t -> p (n t)"),
+            )
+            multiply(1, 3, False, True, bank=3 + h, first=h * H, count=H)
+            nc.scalar.activation(out=y[:, 3 * C + h * H : 3 * C + (h + 1) * H], in_=acc[3 + h][:, 0:H], func=act.Identity, bias=b_sb[:, 3:4])
 
         part1 = held.tile([P, T], F32, name="part1")
         part2 = held.tile([P, T], F32, name="part2")

@@ -21,7 +21,7 @@ SCALAR_SHARE = 256
 LAST = 256
 H = C // 2
 LOAD_ORDER = ((1, 0), (0, 0), (1, 1), (0, 1), (1, 2), (0, 2), (1, 3), (0, 3))
-EARLY = 128
+EARLY = 192
 
 
 def tile_routed_moe_kernel(tc, xT, w_words, w_scales, b, gate, offs, pos1, pos2, out):
@@ -40,8 +40,8 @@ def tile_routed_moe_kernel(tc, xT, w_words, w_scales, b, gate, offs, pos1, pos2,
             planes[(g, t)] = held.tile([P, T], F32, name="plane%d%d" % (g, t), tag="late" if (g, t) == (1, PACK - 1) else "plane%d%d" % (g, t), align_bytes=64)
             if (g, t) == LOAD_ORDER[0]:
                 nc.sync.dma_start(planes[(g, t)][:, 0:SCALAR_SHARE], x_planes[g, :, t, 0:SCALAR_SHARE])
-                nc.sync.dma_start(planes[(g, t)][:, SCALAR_SHARE:T], x_planes[g, :, t, SCALAR_SHARE:T])
                 nc.sync.dma_start(offs_sb[:], offs)
+                nc.sync.dma_start(planes[(g, t)][:, SCALAR_SHARE:T], x_planes[g, :, t, SCALAR_SHARE:T])
             else:
                 nc.sync.dma_start(planes[(g, t)][:], x_planes[g, :, t, :])
 

@@ -45,15 +45,6 @@ def tile_routed_moe_kernel(tc, xT, w_words, w_scales, b, gate, offs, pos1, pos2,
             else:
                 nc.sync.dma_start(planes[(g, t)][:], x_planes[g, :, t, :])
 
-        w_code_sb = held.tile([P, E * PASSES, N * PACK], U8, name="w_code_sb", align_bytes=64)
-        nc.sync.dma_start(w_code_sb[:], w_words.rearrange("e a p n r -> p (e a) (n r)"))
-
-        w_scale_sb = held.tile([P, E * PASSES, N], U8, name="w_scale_sb", align_bytes=64)
-        nc.vector.memset(w_scale_sb[:].rearrange("p j n -> p (j n)").bitcast(I32), 0)
-        scale_rows = w_scales.rearrange("e a (q r) n -> q r (e a) n", r=4)
-        for q in range(4):
-            nc.sync.dma_start(w_scale_sb[32 * q : 32 * q + 4, :, :].bitcast(I32), scale_rows[q].bitcast(I32))
-
         b_sb = held.tile([P, E], F32, name="b_sb")
         nc.sync.dma_start(b_sb[:], b)
         pos1_sb = held.tile([P, T // 16], U16, name="pos1_sb")
@@ -64,6 +55,15 @@ def tile_routed_moe_kernel(tc, xT, w_words, w_scales, b, gate, offs, pos1, pos2,
         nc.sync.dma_start(gate1_sb[:], gate[0])
         gate2_sb = held.tile([P, T], F32, name="gate2_sb")
         nc.sync.dma_start(gate2_sb[:], gate[1])
+
+        w_code_sb = held.tile([P, E * PASSES, N * PACK], U8, name="w_code_sb", align_bytes=64)
+        nc.sync.dma_start(w_code_sb[:], w_words.rearrange("e a p n r -> p (e a) (n r)"))
+
+        w_scale_sb = held.tile([P, E * PASSES, N], U8, name="w_scale_sb", align_bytes=64)
+        nc.vector.memset(w_scale_sb[:].rearrange("p j n -> p (j n)").bitcast(I32), 0)
+        scale_rows = w_scales.rearrange("e a (q r) n -> q r (e a) n", r=4)
+        for q in range(4):
+            nc.sync.dma_start(w_scale_sb[32 * q : 32 * q + 4, :, :].bitcast(I32), scale_rows[q].bitcast(I32))
 
         x_codes = held.tile([P, PASSES, E * C], U32, name="x_codes", align_bytes=64)
         x_scales = held.tile([P, PASSES, E * C], U8, name="x_scales", align_bytes=64)

@@ -21,7 +21,8 @@ SCALAR_SHARE = 256
 LAST = 256
 H = C // 2
 LOAD_ORDER = ((1, 0), (0, 0), (1, 1), (0, 1), (1, 2), (0, 2), (1, 3), (0, 3))
-EARLY = 192
+EARLY = 128
+LATE = 64
 
 
 def tile_routed_moe_kernel(tc, xT, w_words, w_scales, b, gate, offs, pos1, pos2, out):
@@ -131,8 +132,12 @@ def tile_routed_moe_kernel(tc, xT, w_words, w_scales, b, gate, offs, pos1, pos2,
             for t in range(2):
                 nc.scalar.activation(pairs0[:, e - 2, 1, :, t], rounded0[:, t, :].indirect(slots(e)), act.Copy)
         pairs13 = held.tile([P, 2, C, 2], BF16, name="pairs13", tag="plane00", align_bytes=64)
+        for t in range(2):
+            nc.vector.tensor_copy(pairs13[:, 0, 0:LATE, t], planes[(1, t)][:].indirect(offs_sb[:, 3 * OFFS_COLS : 3 * OFFS_COLS + LATE // 16]))
         for t in range(PACK):
-            if t == PACK - 1:
+            if t < 2:
+                nc.scalar.activation(pairs13[:, 0, LATE:C, t], rounded1[:, t, :].indirect(offs_sb[:, 3 * OFFS_COLS + LATE // 16 : 4 * OFFS_COLS]), act.Copy)
+            elif t == PACK - 1:
                 for h in range(2):
                     nc.scalar.activation(
                         pairs13[:, t // 2, h * H : (h + 1) * H, t % 2],

@@ -103,26 +103,25 @@ def tile_routed_moe_kernel(tc, xT, w_words, w_scales, b, gate, offs, pos1, pos2,
             elif t >= 2:
                 round_on_gpsimd(rounded0[:, t - 2, :], planes[(g, t)][:])
 
-        pairs12 = held.tile([P, 2, C, 2], BF16, name="pairs12", align_bytes=64)
+        pairs012 = held.tile([P, 2, 3 * C, 2], BF16, name="pairs012", align_bytes=64)
         for t in range(2):
-            nc.vector.tensor_copy(pairs12[:, 0, 0:EARLY, t], planes[(1, t)][:].indirect(offs_sb[:, 2 * OFFS_COLS : 2 * OFFS_COLS + EARLY // 16]))
+            nc.vector.tensor_copy(pairs012[:, 0, 2 * C : 2 * C + EARLY, t], planes[(1, t)][:].indirect(offs_sb[:, 2 * OFFS_COLS : 2 * OFFS_COLS + EARLY // 16]))
 
-        picked = [held.tile([P, PACK, C], F32, name="picked%d" % e, align_bytes=64) for e in range(2)]
+        picked = held.tile([P, 2, PACK, C], F32, name="picked", align_bytes=64)
         for t in range(PACK):
             for e in range(2):
-                nc.vector.tensor_copy(picked[e][:, t, :], planes[(0, t)][:].indirect(slots(e)))
+                nc.vector.tensor_copy(picked[:, e, t, :], planes[(0, t)][:].indirect(slots(e)))
         grouped_a = held.tile([P, 2 * C, PACK], BF16, name="grouped_a", align_bytes=64)
         for e in range(2):
-            round_on_gpsimd(grouped_a[:, e * C : (e + 1) * C, :], picked[e][:].rearrange("p t n -> p n t"))
+            round_on_gpsimd(grouped_a[:, e * C : (e + 1) * C, :], picked[:, e].rearrange("p t n -> p n t"))
 
         pairs0 = held.tile([P, 2, 2, C, 2], BF16, name="pairs0", tag="late", align_bytes=64)
         for e in (2, 3):
             for t in range(2):
                 nc.vector.tensor_copy(pairs0[:, e - 2, 0, :, t], planes[(0, t)][:].indirect(slots(e)))
 
-        pairs01 = held.tile([P, 2, 2, C, 2], BF16, name="pairs01", align_bytes=64)
         for e in range(3):
-            pairs = pairs01[:, e] if e < 2 else pairs12[:]
+            pairs = pairs012[:, :, e * C : (e + 1) * C, :]
             for t in range(PACK):
                 if e == 2 and t < 2:
                     nc.scalar.activation(pairs[:, 0, EARLY:C, t], rounded1[:, t, :].indirect(offs_sb[:, 2 * OFFS_COLS + EARLY // 16 : 3 * OFFS_COLS]), act.Copy)
@@ -159,18 +158,16 @@ def tile_routed_moe_kernel(tc, xT, w_words, w_scales, b, gate, offs, pos1, pos2,
         quantize(0, 0, 2, grouped_a[:].rearrange("p n t -> p (n t)"))
         multiply(0, 0, True, False)
         multiply(0, 1, True, False)
-        merged01 = held.tile([P, 2 * C, PACK], BF16, name="merged01", tag="picked1", align_bytes=64)
-        merge_two(merged01[:], pairs01[:])
-        quantize(1, 0, 2, merged01[:].rearrange("p n t -> p (n t)"))
+        merged012 = held.tile([P, 3 * C, PACK], BF16, name="merged012", tag="picked", align_bytes=64)
+        nc.vector.tensor_copy(
+            out=merged012[:].rearrange("p n t -> p (n t)").bitcast(F32).rearrange("p (n u) -> p n u", u=2),
+            in_=pairs012[:].rearrange("p u n i -> p (u n i)").bitcast(F32).rearrange("p (u n) -> p n u", u=2),
+        )
+        quantize(1, 0, 2, merged012[:, 0 : 2 * C, :].rearrange("p n t -> p (n t)"))
         for e in range(2):
             multiply(1, e, False, True)
             read_bank(e)
-        merged12 = held.tile([P, C, PACK], BF16, name="merged12", tag="picked0", align_bytes=64)
-        nc.vector.tensor_copy(
-            out=merged12[:].rearrange("p n t -> p (n t)").bitcast(F32).rearrange("p (n u) -> p n u", u=2),
-            in_=pairs12[:].rearrange("p u n i -> p (u n i)").bitcast(F32).rearrange("p (u n) -> p n u", u=2),
-        )
-        quantize(1, 2, 1, merged12[:].rearrange("p n t -> p (n t)"))
+        quantize(1, 2, 1, merged012[:, 2 * C : 3 * C, :].rearrange("p n t -> p (n t)"))
         multiply(1, 2, True, False)
         merged023 = held.tile([P, 2 * C, PACK], BF16, name="merged023", tag="grouped_a", align_bytes=64)
         merge_two(merged023[:], pairs0[:])
@@ -179,7 +176,7 @@ def tile_routed_moe_kernel(tc, xT, w_words, w_scales, b, gate, offs, pos1, pos2,
         read_bank(2)
         for h in range(2):
             multiply(0, 3, True, False, bank=3 + h, first=h * H, count=H)
-        merged13 = held.tile([P, C, PACK], BF16, name="merged13", tag="picked1", align_bytes=64)
+        merged13 = held.tile([P, C, PACK], BF16, name="merged13", tag="picked", align_bytes=64)
         for h in range(2):
             part = slice(h * H, (h + 1) * H)
             nc.vector.tensor_copy(

@@ -107,13 +107,16 @@ def tile_routed_moe_kernel(tc, xT, w_words, w_scales, b, gate, offs, pos1, pos2,
         for t in range(2):
             nc.vector.tensor_copy(pairs012[:, 0, 2 * C : 2 * C + EARLY, t], planes[(1, t)][:].indirect(offs_sb[:, 2 * OFFS_COLS : 2 * OFFS_COLS + EARLY // 16]))
 
-        picked = held.tile([P, 2, PACK, C], F32, name="picked", align_bytes=64)
+        picked = held.tile([P, 2, 2 * C, 2], BF16, name="picked", align_bytes=64)
         for t in range(PACK):
             for e in range(2):
-                nc.vector.tensor_copy(picked[:, e, t, :], planes[(0, t)][:].indirect(slots(e)))
+                nc.vector.tensor_copy(picked[:, t // 2, e * C : (e + 1) * C, t % 2], planes[(0, t)][:].indirect(slots(e)))
         grouped_a = held.tile([P, 2 * C, PACK], BF16, name="grouped_a", align_bytes=64)
         for e in range(2):
-            round_on_gpsimd(grouped_a[:, e * C : (e + 1) * C, :], picked[:, e].rearrange("p t n -> p n t"))
+            nc.gpsimd.tensor_copy(
+                out=grouped_a[:, e * C : (e + 1) * C, :].rearrange("p n t -> p (n t)").bitcast(F32).rearrange("p (n u) -> p n u", u=2),
+                in_=picked[:, :, e * C : (e + 1) * C, :].rearrange("p u n i -> p u (n i)").bitcast(F32).rearrange("p u n -> p n u"),
+            )
 
         pairs0 = held.tile([P, 2, 2, C, 2], BF16, name="pairs0", tag="late", align_bytes=64)
         for e in (2, 3):

@@ -21,7 +21,7 @@ SCALAR_SHARE = 256
 LAST = 256
 H = C // 2
 LOAD_ORDER = ((1, 0), (0, 0), (1, 1), (0, 1), (1, 2), (0, 2), (1, 3), (0, 3))
-EARLY = 128
+EARLY = 256
 LATE = 64
 
 
@@ -126,6 +126,8 @@ def tile_routed_moe_kernel(tc, xT, w_words, w_scales, b, gate, offs, pos1, pos2,
         for e in range(3):
             pairs = pairs012[:, :, e * C : (e + 1) * C, :]
             for t in range(PACK):
+                if e == 2 and t < 2 and EARLY == C:
+                    continue
                 if e == 2 and t < 2:
                     nc.scalar.activation(pairs[:, 0, EARLY:C, t], rounded1[:, t, :].indirect(offs_sb[:, 2 * OFFS_COLS + EARLY // 16 : 3 * OFFS_COLS]), act.Copy)
                 else:
@@ -162,10 +164,11 @@ def tile_routed_moe_kernel(tc, xT, w_words, w_scales, b, gate, offs, pos1, pos2,
         multiply(0, 0, True, False)
         multiply(0, 1, True, False)
         merged012 = held.tile([P, 3 * C, PACK], BF16, name="merged012", tag="picked", align_bytes=64)
-        nc.vector.tensor_copy(
-            out=merged012[:].rearrange("p n t -> p (n t)").bitcast(F32).rearrange("p (n u) -> p n u", u=2),
-            in_=pairs012[:].rearrange("p u n i -> p (u n i)").bitcast(F32).rearrange("p (u n) -> p n u", u=2),
-        )
+        for e, engine in enumerate((nc.gpsimd, nc.gpsimd, nc.vector)):
+            engine.tensor_copy(
+                out=merged012[:, e * C : (e + 1) * C, :].rearrange("p n t -> p (n t)").bitcast(F32).rearrange("p (n u) -> p n u", u=2),
+                in_=pairs012[:, :, e * C : (e + 1) * C, :].rearrange("p u n i -> p u (n i)").bitcast(F32).rearrange("p u n -> p n u"),
+            )
         quantize(1, 0, 2, merged012[:, 0 : 2 * C, :].rearrange("p n t -> p (n t)"))
         for e in range(2):
             multiply(1, e, False, True)

@@ -41,8 +41,8 @@ def tile_routed_moe_kernel(tc, xT, w_words, w_scales, b, gate, offs, pos1, pos2,
             planes[(g, t)] = held.tile([P, T], F32, name="plane%d%d" % (g, t), tag="late" if (g, t) == (1, PACK - 1) else "plane%d%d" % (g, t), align_bytes=64)
             if (g, t) == LOAD_ORDER[0]:
                 nc.sync.dma_start(planes[(g, t)][:, 0:SCALAR_SHARE], x_planes[g, :, t, 0:SCALAR_SHARE])
-                nc.sync.dma_start(offs_sb[:], offs)
                 nc.sync.dma_start(planes[(g, t)][:, SCALAR_SHARE:T], x_planes[g, :, t, SCALAR_SHARE:T])
+                nc.sync.dma_start(offs_sb[:], offs)
             else:
                 nc.sync.dma_start(planes[(g, t)][:], x_planes[g, :, t, :])
 

@@ -206,6 +206,6 @@ def tile_routed_moe_kernel(tc, xT, w_words, w_scales, b, gate, offs, pos1, pos2,
         pieces = (slice(0, T - LAST), slice(T - LAST, T))
         for cols in pieces:
             nc.vector.tensor_tensor(out=part2[:, cols], in0=y[:].indirect(pos2_sb[:, cols.start // 16 : cols.stop // 16]), in1=gate2_sb[:, cols], op=mult)
-        for cols, queue in zip(pieces, (nc.sync, nc.scalar)):
+        for cols, queue in zip(pieces, (nc.sync, nc.sync)):
             nc.vector.tensor_tensor(out=result[:, cols], in0=part1[:, cols], in1=part2[:, cols], op=add)
             queue.dma_start(out[:, cols], result[:, cols])

@@ -77,7 +77,7 @@ def tile_routed_moe_kernel(tc, xT, w_words, w_scales, b, gate, offs, pos1, pos2,
             return offs_sb[:, e * OFFS_COLS : (e + 1) * OFFS_COLS]
 
         def round_on_gpsimd(dst, src):
-            nc.gpsimd.tensor_scalar(out=dst, in0=src, scalar1=1.0, scalar2=0.0, op0=mult, op1=add)
+            nc.gpsimd.tensor_copy(out=dst, in_=src)
 
         def quantize(g, first, count, in_):
             cols = slice(first * C, (first + count) * C)
@@ -163,17 +163,18 @@ def tile_routed_moe_kernel(tc, xT, w_words, w_scales, b, gate, offs, pos1, pos2,
         quantize(0, 0, 2, grouped_a[:].rearrange("p n t -> p (n t)"))
         multiply(0, 0, True, False)
         multiply(0, 1, True, False)
-        merged012 = held.tile([P, 3 * C, PACK], BF16, name="merged012", tag="picked", align_bytes=64)
-        for e, engine in enumerate((nc.gpsimd, nc.gpsimd, nc.vector)):
+        merged01 = held.tile([P, 2 * C, PACK], BF16, name="merged01", align_bytes=64)
+        merged2 = held.tile([P, C, PACK], BF16, name="merged2", tag="picked", align_bytes=64)
+        for e, engine, dst in ((0, nc.gpsimd, merged01[:, 0:C, :]), (1, nc.gpsimd, merged01[:, C : 2 * C, :]), (2, nc.vector, merged2[:])):
             engine.tensor_copy(
-                out=merged012[:, e * C : (e + 1) * C, :].rearrange("p n t -> p (n t)").bitcast(F32).rearrange("p (n u) -> p n u", u=2),
+                out=dst.rearrange("p n t -> p (n t)").bitcast(F32).rearrange("p (n u) -> p n u", u=2),
                 in_=pairs012[:, :, e * C : (e + 1) * C, :].rearrange("p u n i -> p u (n i)").bitcast(F32).rearrange("p u n -> p n u"),
             )
-        quantize(1, 0, 2, merged012[:, 0 : 2 * C, :].rearrange("p n t -> p (n t)"))
+        quantize(1, 0, 2, merged01[:].rearrange("p n t -> p (n t)"))
         for e in range(2):
             multiply(1, e, False, True)
             read_bank(e)
-        quantize(1, 2, 1, merged012[:, 2 * C : 3 * C, :].rearrange("p n t -> p (n t)"))
+        quantize(1, 2, 1, merged2[:].rearrange("p n t -> p (n t)"))
         multiply(1, 2, True, False)
         merged023 = held.tile([P, 2 * C, PACK], BF16, name="merged023", tag="grouped_a", align_bytes=64)
         merge_two(merged023[:], pairs0[:])

@@ -46,6 +46,12 @@ def tile_routed_moe_kernel(tc, xT, w_words, w_scales, b, gate, offs, pos1, pos2,
             else:
                 nc.sync.dma_start(planes[(g, t)][:], x_planes[g, :, t, :])
 
+        w_scale_sb = held.tile([P, E * PASSES, N], U8, name="w_scale_sb", align_bytes=64)
+        nc.vector.memset(w_scale_sb[:].rearrange("p j n -> p (j n)").bitcast(I32), 0)
+        scale_rows = w_scales.rearrange("e a (q r) n -> q r (e a) n", r=4)
+        for q in range(4):
+            nc.sync.dma_start(w_scale_sb[32 * q : 32 * q + 4, :, :].bitcast(I32), scale_rows[q].bitcast(I32))
+
         b_sb = held.tile([P, E], F32, name="b_sb")
         nc.sync.dma_start(b_sb[:], b)
         pos1_sb = held.tile([P, T // 16], U16, name="pos1_sb")
@@ -60,11 +66,6 @@ def tile_routed_moe_kernel(tc, xT, w_words, w_scales, b, gate, offs, pos1, pos2,
         w_code_sb = held.tile([P, E * PASSES, N * PACK], U8, name="w_code_sb", align_bytes=64)
         nc.sync.dma_start(w_code_sb[:], w_words.rearrange("e a p n r -> p (e a) (n r)"))
 
-        w_scale_sb = held.tile([P, E * PASSES, N], U8, name="w_scale_sb", align_bytes=64)
-        nc.vector.memset(w_scale_sb[:].rearrange("p j n -> p (j n)").bitcast(I32), 0)
-        scale_rows = w_scales.rearrange("e a (q r) n -> q r (e a) n", r=4)
-        for q in range(4):
-            nc.sync.dma_start(w_scale_sb[32 * q : 32 * q + 4, :, :].bitcast(I32), scale_rows[q].bitcast(I32))
 
         x_codes = held.tile([P, PASSES, E * C], U32, name="x_codes", align_bytes=64)
         x_scales = held.tile([P, PASSES, E * C], U8, name="x_scales", align_bytes=64)

from contextlib import ExitStack

import concourse.mybir as mybir

K, T, E, C, N = 1024, 512, 4, 256, 128
FLOPS = 2 * K * N * E * C

F32 = mybir.dt.float32
BF16 = mybir.dt.bfloat16
U8 = mybir.dt.uint8
U16 = mybir.dt.uint16
U32 = mybir.dt.uint32
I32 = mybir.dt.int32
FP8X4 = mybir.dt.float8_e4m3fn_x4

P = 128
PACK = 4
PASSES = K // (P * PACK)
OFFS_COLS = C // 16
SCALAR_SHARE = 256
LAST = 256
H = C // 2
LOAD_ORDER = ((1, 0), (0, 0), (1, 1), (0, 1), (1, 2), (0, 2), (1, 3), (0, 3))
EARLY = 256
LATE = 64


def tile_routed_moe_kernel(tc, xT, w_words, w_scales, b, gate, offs, pos1, pos2, out):
    nc = tc.nc
    mult, add = mybir.AluOpType.mult, mybir.AluOpType.add
    act = mybir.ActivationFunctionType
    with ExitStack() as ctx:
        held = ctx.enter_context(tc.tile_pool(name="held", bufs=1))
        psum = ctx.enter_context(tc.psum_pool(name="psum", bufs=1))

        offs_sb = held.tile([P, E * C // 16], U16, name="offs_sb")

        x_planes = xT.rearrange("(g p t) n -> g p t n", p=P, t=PACK)
        planes = {}
        for g, t in LOAD_ORDER:
            planes[(g, t)] = held.tile([P, T], F32, name="plane%d%d" % (g, t), tag="late" if (g, t) == (1, PACK - 1) else "plane%d%d" % (g, t), align_bytes=64)
            if (g, t) == LOAD_ORDER[0]:
                nc.sync.dma_start(planes[(g, t)][:, 0:SCALAR_SHARE], x_planes[g, :, t, 0:SCALAR_SHARE])
                nc.sync.dma_start(planes[(g, t)][:, SCALAR_SHARE:T], x_planes[g, :, t, SCALAR_SHARE:T])
                nc.sync.dma_start(offs_sb[:], offs)
            else:
                nc.sync.dma_start(planes[(g, t)][:], x_planes[g, :, t, :])

        w_scale_sb = held.tile([P, E * PASSES, N], U8, name="w_scale_sb", align_bytes=64)
        nc.vector.memset(w_scale_sb[:].rearrange("p j n -> p (j n)").bitcast(I32), 0)
        scale_rows = w_scales.rearrange("e a (q r) n -> q r (e a) n", r=4)
        for q in range(4):
            nc.sync.dma_start(w_scale_sb[32 * q : 32 * q + 4, :, :].bitcast(I32), scale_rows[q].bitcast(I32))

        b_sb = held.tile([P, E], F32, name="b_sb")
        nc.sync.dma_start(b_sb[:], b)
        pos1_sb = held.tile([P, T // 16], U16, name="pos1_sb")
        nc.sync.dma_start(pos1_sb[:], pos1)
        pos2_sb = held.tile([P, T // 16], U16, name="pos2_sb")
        nc.sync.dma_start(pos2_sb[:], pos2)
        gate1_sb = held.tile([P, T], F32, name="gate1_sb")
        nc.sync.dma_start(gate1_sb[:], gate[0])
        gate2_sb = held.tile([P, T], F32, name="gate2_sb")
        nc.sync.dma_start(gate2_sb[:], gate[1])

        w_code_sb = held.tile([P, E * PASSES, N * PACK], U8, name="w_code_sb", align_bytes=64)
        nc.sync.dma_start(w_code_sb[:], w_words.rearrange("e a p n r -> p (e a) (n r)"))


        x_codes = held.tile([P, PASSES, E * C], U32, name="x_codes", align_bytes=64)
        x_scales = held.tile([P, PASSES, E * C], U8, name="x_scales", align_bytes=64)
        y = held.tile([P, E * C], F32, name="y")
        acc = [psum.tile([P, 512], F32, name="acc%d" % e) for e in range(E + 1)]
        rounded1 = held.tile([P, PACK, T], BF16, name="rounded1")
        rounded0 = held.tile([P, 2, T], BF16, name="rounded0")

        def slots(e):
            return offs_sb[:, e * OFFS_COLS : (e + 1) * OFFS_COLS]

        def round_on_gpsimd(dst, src):
            nc.gpsimd.tensor_copy(out=dst, in_=src)

        def quantize(g, first, count, in_):
            cols = slice(first * C, (first + count) * C)
            nc.vector.quantize_mx(out=x_codes[:, g, cols].bitcast(FP8X4), scales=x_scales[:, g, cols], in_=in_)

        def multiply(g, e, start, stop, bank=None, first=0, count=C):
            cols = slice(e * C + first, e * C + first + count)
            nc.tensor.matmul_mx(
                out=acc[e if bank is None else bank][:, 0:count],
                lhsT=w_code_sb[:, e * PASSES + g, :].bitcast(FP8X4),
                lhsT_scale=w_scale_sb[:, e * PASSES + g, :],
                rhs=x_codes[:, g, cols].bitcast(FP8X4),
                rhs_scale=x_scales[:, g, cols],
                start=start,
                stop=stop,
            )

        nc.scalar.copy(out=rounded1[:, 0, 0:SCALAR_SHARE], in_=planes[(1, 0)][:, 0:SCALAR_SHARE])
        nc.vector.tensor_copy(out=rounded1[:, 0, SCALAR_SHARE:T], in_=planes[(1, 0)][:, SCALAR_SHARE:T])
        for g, t in LOAD_ORDER[1:]:
            if g == 1:
                round_on_gpsimd(rounded1[:, t, :], planes[(g, t)][:])
            elif t >= 2:
                round_on_gpsimd(rounded0[:, t - 2, :], planes[(g, t)][:])

        pairs012 = held.tile([P, 2, 3 * C, 2], BF16, name="pairs012", align_bytes=64)
        for t in range(2):
            nc.vector.tensor_copy(pairs012[:, 0, 2 * C : 2 * C + EARLY, t], planes[(1, t)][:].indirect(offs_sb[:, 2 * OFFS_COLS : 2 * OFFS_COLS + EARLY // 16]))

        picked = held.tile([P, 2, 2 * C, 2], BF16, name="picked", align_bytes=64)
        for t in range(PACK):
            for e in range(2):
                nc.vector.tensor_copy(picked[:, t // 2, e * C : (e + 1) * C, t % 2], planes[(0, t)][:].indirect(slots(e)))
        grouped_a = held.tile([P, 2 * C, PACK], BF16, name="grouped_a", align_bytes=64)
        for e in range(2):
            nc.gpsimd.tensor_copy(
                out=grouped_a[:, e * C : (e + 1) * C, :].rearrange("p n t -> p (n t)").bitcast(F32).rearrange("p (n u) -> p n u", u=2),
                in_=picked[:, :, e * C : (e + 1) * C, :].rearrange("p u n i -> p u (n i)").bitcast(F32).rearrange("p u n -> p n u"),
            )

        pairs0 = held.tile([P, 2, 2, C, 2], BF16, name="pairs0", tag="late", align_bytes=64)
        for e in (2, 3):
            for t in range(2):
                nc.vector.tensor_copy(pairs0[:, e - 2, 0, :, t], planes[(0, t)][:].indirect(slots(e)))

        for e in range(3):
            pairs = pairs012[:, :, e * C : (e + 1) * C, :]
            for t in range(PACK):
                if e == 2 and t < 2 and EARLY == C:
                    continue
                if e == 2 and t < 2:
                    nc.scalar.activation(pairs[:, 0, EARLY:C, t], rounded1[:, t, :].indirect(offs_sb[:, 2 * OFFS_COLS + EARLY // 16 : 3 * OFFS_COLS]), act.Copy)
                else:
                    nc.scalar.activation(pairs[:, t // 2, :, t % 2], rounded1[:, t, :].indirect(slots(e)), act.Copy)
        for e in (2, 3):
            for t in range(2):
                nc.scalar.activation(pairs0[:, e - 2, 1, :, t], rounded0[:, t, :].indirect(slots(e)), act.Copy)
        pairs13 = held.tile([P, 2, C, 2], BF16, name="pairs13", tag="plane00", align_bytes=64)
        for t in range(2):
            nc.vector.tensor_copy(pairs13[:, 0, 0:LATE, t], planes[(1, t)][:].indirect(offs_sb[:, 3 * OFFS_COLS : 3 * OFFS_COLS + LATE // 16]))
        for t in range(PACK):
            if t < 2:
                nc.scalar.activation(pairs13[:, 0, LATE:C, t], rounded1[:, t, :].indirect(offs_sb[:, 3 * OFFS_COLS + LATE // 16 : 4 * OFFS_COLS]), act.Copy)
            elif t == PACK - 1:
                for h in range(2):
                    nc.scalar.activation(
                        pairs13[:, t // 2, h * H : (h + 1) * H, t % 2],
                        rounded1[:, t, :].indirect(offs_sb[:, 3 * OFFS_COLS + h * H // 16 : 3 * OFFS_COLS + (h + 1) * H // 16]),
                        act.Copy,
                    )
            else:
                nc.scalar.activation(pairs13[:, t // 2, :, t % 2], rounded1[:, t, :].indirect(slots(3)), act.Copy)

        def merge_two(dst, src):
            nc.vector.tensor_copy(
                out=dst.rearrange("p n t -> p (n t)").bitcast(F32).rearrange("p (a n u) -> p a n u", a=2, u=2),
                in_=src.rearrange("p a u n i -> p (a u n i)").bitcast(F32).rearrange("p (a u n) -> p a n u", a=2, u=2),
            )

        def read_bank(e):
            nc.scalar.activation(out=y[:, e * C : (e + 1) * C], in_=acc[e][:, 0:C], func=act.Identity, bias=b_sb[:, e : e + 1])

        quantize(0, 0, 2, grouped_a[:].rearrange("p n t -> p (n t)"))
        multiply(0, 0, True, False)
        multiply(0, 1, True, False)
        merged01 = held.tile([P, 2 * C, PACK], BF16, name="merged01", align_bytes=64)
        merged2 = held.tile([P, C, PACK], BF16, name="merged2", tag="picked", align_bytes=64)
        for e, engine, dst in ((0, nc.gpsimd, merged01[:, 0:C, :]), (1, nc.gpsimd, merged01[:, C : 2 * C, :]), (2, nc.vector, merged2[:])):
            engine.tensor_copy(
                out=dst.rearrange("p n t -> p (n t)").bitcast(F32).rearrange("p (n u) -> p n u", u=2),
                in_=pairs012[:, :, e * C : (e + 1) * C, :].rearrange("p u n i -> p u (n i)").bitcast(F32).rearrange("p u n -> p n u"),
            )
        quantize(1, 0, 2, merged01[:].rearrange("p n t -> p (n t)"))
        for e in range(2):
            multiply(1, e, False, True)
            read_bank(e)
        quantize(1, 2, 1, merged2[:].rearrange("p n t -> p (n t)"))
        multiply(1, 2, True, False)
        merged023 = held.tile([P, 2 * C, PACK], BF16, name="merged023", tag="grouped_a", align_bytes=64)
        merge_two(merged023[:], pairs0[:])
        quantize(0, 2, 2, merged023[:].rearrange("p n t -> p (n t)"))
        multiply(0, 2, False, True)
        read_bank(2)
        for h in range(2):
            multiply(0, 3, True, False, bank=3 + h, first=h * H, count=H)
        merged13 = held.tile([P, C, PACK], BF16, name="merged13", tag="picked", align_bytes=64)
        for h in range(2):
            part = slice(h * H, (h + 1) * H)
            nc.vector.tensor_copy(
                out=merged13[:, part, :].rearrange("p n t -> p (n t)").bitcast(F32).rearrange("p (n u) -> p n u", u=2),
                in_=pairs13[:, :, part, :].rearrange("p u n i -> p u (n i)").bitcast(F32).rearrange("p u n -> p n u"),
            )
        for h in range(2):
            part = slice(h * H, (h + 1) * H)
            nc.vector.quantize_mx(
                out=x_codes[:, 1, 3 * C + h * H : 3 * C + (h + 1) * H].bitcast(FP8X4),
                scales=x_scales[:, 1, 3 * C + h * H : 3 * C + (h + 1) * H],
                in_=merged13[:, part, :].rearrange("p n t -> p (n t)"),
            )
            multiply(1, 3, False, True, bank=3 + h, first=h * H, count=H)
            nc.scalar.activation(out=y[:, 3 * C + h * H : 3 * C + (h + 1) * H], in_=acc[3 + h][:, 0:H], func=act.Identity, bias=b_sb[:, 3:4])

        part1 = held.tile([P, T], F32, name="part1")
        part2 = held.tile([P, T], F32, name="part2")
        result = held.tile([P, T], F32, name="result")
        nc.vector.tensor_tensor(out=part1[:], in0=y[:].indirect(pos1_sb[:]), in1=gate1_sb[:], op=mult)
        pieces = (slice(0, T - LAST), slice(T - LAST, T))
        for cols in pieces:
            nc.vector.tensor_tensor(out=part2[:, cols], in0=y[:].indirect(pos2_sb[:, cols.start // 16 : cols.stop // 16]), in1=gate2_sb[:, cols], op=mult)
        for cols, queue in zip(pieces, (nc.sync, nc.sync)):
            nc.vector.tensor_tensor(out=result[:, cols], in0=part1[:, cols], in1=part2[:, cols], op=add)
            queue.dma_start(out[:, cols], result[:, cols])
